import numpy as np, ml_dtypes
CORES = [2,3,42,43,82,83,122,123]
N = 8
import mx_ref
BF = ml_dtypes.bfloat16
def entries(a):
    return np.ascontiguousarray(a.T).reshape(-1)
def table(e):
    return np.ascontiguousarray(np.reshape(e, (-1, 16)).T).astype(np.int32)
def f(rng, *shape):
    return mx_ref.flush((rng.standard_normal(shape, dtype=np.float32) * np.exp2(rng.integers(-2, 3, shape[:-1] + (1,)))).astype(BF))
def wide(rng, *shape, cols=0):
    v = rng.standard_normal(shape, dtype=np.float32) * np.exp2(rng.integers(-12, 13, shape)).astype(np.float32)
    if cols: v *= np.repeat(np.exp2(rng.integers(-cols, cols + 1, shape[:-2] + (1, shape[-1] // 4))) * (rng.random(shape[:-2] + (1, shape[-1] // 4)) > 0.0625), 4, axis=-1).astype(np.float32)
    return mx_ref.flush(v.astype(BF))
R, P, MOST = 5, 64, 5
def lists(rng, plan, tie=False):
    v = rng.integers(0, 1001, (N, R, P))
    hold = np.arange(P).reshape(N, 8)
    for t in range(R):
        for a in range(t % 2, N - 1, 2):
            A, B, go = v[a, t], v[a + 1, t], set(int(k) for k in plan(t, a))
            for k in range(8):
                p, q = int(hold[a, k]), int(hold[a + 1, k])
                if tie:
                    A[[p, q]] = rng.integers(300, 701, 2)
                    B[[p, q]] = A[[p, q]] + rng.integers(-200, 201)
                    if k in go: A[q] += 1
                else:
                    while A[q] + B[p] == A[p] + B[q]:
                        A[[p, q]] = rng.integers(0, 1001, 2)
                        B[[p, q]] = rng.integers(0, 1001, 2)
                    if (A[q] + B[p] > A[p] + B[q]) != (k in go):
                        A[[p, q]] = A[[q, p]]
                        B[[p, q]] = B[[q, p]]
                if k in go: hold[a, k], hold[a + 1, k] = q, p
    return {"dm": np.stack([table(e.reshape(-1)) for e in v])}
def setup_inputs(rng):
    return {"x": f(rng, N, 128, 512 * R), "w": f(rng, N, 128, 1024), **lists(rng, lambda t, a: rng.permutation(8)[:rng.integers(0, MOST + 1)])}
def setup_inputs_back(rng):
    go = rng.permutation(8)[:MOST]
    return {**setup_inputs(rng), **lists(rng, lambda t, a: [] if t % 2 else go)}
def setup_inputs_carry(rng):
    d = setup_inputs(rng)
    go = rng.permutation(8)[:MOST]
    c = rng.permutation(np.repeat([-5, 5], 4))
    e = np.where(np.arange(N)[:, None] % 2 == 0, c, -c)
    s = np.exp2(e).astype(np.float32)[:, None, :, None]
    d["w"] = mx_ref.flush((d["w"].astype(np.float32).reshape(N, 128, 8, 128) * s).reshape(N, 128, 1024).astype(BF))
    return {**d, **lists(rng, lambda t, a: go)}
def setup_inputs_equal(rng):
    return {**setup_inputs(rng), **lists(rng, lambda t, a: rng.permutation(8)[:MOST], tie=True)}
def setup_inputs_turn(rng):
    go = rng.permutation(8)
    return {**setup_inputs(rng), **lists(rng, lambda t, a: go[:MOST] if t < 2 else go[8 - MOST:])}
def setup_inputs_spread(rng):
    d = setup_inputs(rng); d["x"] = wide(rng, N, 128, 512 * R, cols=6); return d
def rounds(dm):
    v = np.stack([entries(e) for e in dm]).reshape(N, R, P)
    hold = np.arange(P).reshape(N, 8)
    held, most = [], 0
    for t in range(R):
        for a in range(t % 2, N - 1, 2):
            n = 0
            for k in range(8):
                p, q = int(hold[a, k]), int(hold[a + 1, k])
                if v[a, t, q] + v[a + 1, t, p] > v[a, t, p] + v[a + 1, t, q]:
                    hold[a, k], hold[a + 1, k] = q, p
                    n += 1
            most = max(most, n)
        held.append(np.array(hold))
    return held, most
def check_inputs(d):
    for n in ("x", "w"):
        m = np.abs(d[n].astype(np.float32))
        if not np.all((m == 0) | ((m >= 2.0 ** -30) & (m <= 2.0 ** 30))): return [n]
    if d["dm"].min() < 0 or d["dm"].max() > 1000: return ["dm"]
    return ["more than MOST slots change at a pair in a round"] if rounds(d["dm"])[1] > MOST else []
def reference(x, w, dm):
    held = rounds(dm)[0]
    y = np.zeros((N, 128, 256 * R), np.float32)
    for t in range(R):
        for r in range(N):
            X = mx_ref.quantize(np.ascontiguousarray(x[r][:, 512 * t:512 * t + 512]))
            for h in range(2):
                S = np.concatenate([w[p >> 3][:, 128 * (p & 7):128 * (p & 7) + 128] for p in held[t][r, 4 * h:4 * h + 4]], axis=1)
                y[r][:, 256 * t + 128 * h:256 * t + 128 * h + 128] = mx_ref.matmul(mx_ref.quantize(S), X)
    return {"y": y}

@@ -1,0 +1,545 @@
+from concourse.bass import DstId, RemoteDMATransfer
+from concourse.mybir import dt, AluOpType as Op, ActivationFunctionType as Act
+
+C8 = "float8_e4m3fn_x4"
+SCRATCH = {
+    "d3": ("dram", [128, 3], "int32"),
+    "wt": ("sbuf", [128, 1024], "bfloat16"),
+    "xt": ("sbuf", [128, 2560], "bfloat16"),
+    "xq": ("sbuf", [128, 640], C8), "xs": ("sbuf", [128, 640], "uint8"),
+    "hb": ("sbuf", [128, 1024], C8), "hbs": ("sbuf", [128, 1024], "uint8"),
+    "win": ("sbuf", [128, 1536], C8), "wins": ("sbuf", [128, 1536], "uint8"),
+    "pa": ("sbuf", [128, 1024], C8), "pas": ("sbuf", [128, 1024], "uint8"),
+    "hw": ("sbuf", [128, 256], C8), "hws": ("sbuf", [128, 256], "uint8"),
+    "pk": ("sbuf", [128, 1280], C8), "pks": ("sbuf", [128, 1280], "uint8"),
+    "se": ("sbuf", [128, 2, 2, 4, 12], "int32"), "so": ("sbuf", [128, 2, 2, 4, 12], "int32"),
+    "cr": ("sbuf", [128, 4], "float32"),
+    "cp": ("sbuf", [128, 4], "float32"), "ck": ("sbuf", [128, 4], "float32"), "cx": ("sbuf", [128, 4], "float32"),
+    "sab": ("sbuf", [128, 2, 68], "float32"),
+    "e0": ("sbuf", [128, 2, 16], "float32"),
+    "dd": ("sbuf", [128, 64], "float32"), "cd": ("sbuf", [128, 64], "float32"),
+    "ce": ("sbuf", [128, 8], "float32"), "co": ("sbuf", [128, 8], "float32"),
+    "wk": ("sbuf", [128, 32], "float32"),
+    "li": ("sbuf", [128, 12], "float32"), "pp": ("sbuf", [128, 4], "float32"),
+    "pi": ("sbuf", [128, 4], "int32"), "pj": ("sbuf", [128, 4], "int32"), "p3": ("sbuf", [128, 4], "int32"),
+    "ph": ("sbuf", [128, 4], "int32"), "pf": ("sbuf", [128, 2], "float32"),
+    "of": ("sbuf", [128, 4], "uint16"), "oz": ("sbuf", [128, 4], "uint16"),
+    "tt": ("sbuf", [128, 32], "float32"), "tr": ("sbuf", [128, 32], "float32"),
+    "bj": ("sbuf", [128, 8], "float32"), "jl": ("sbuf", [128, 16], "uint16"),
+    "tf": ("sbuf", [128, 64], "float32"), "bf": ("sbuf", [128, 40], "float32"), "lu": ("sbuf", [128, 80], "uint16"),
+    "ys": ("sbuf", [128, 1280], "float32"),
+    "acc": ("psum", [128, 4096], "float32"),
+}
+for _j in range(8):
+    SCRATCH["ld%d" % _j] = ("dram", [128, 3], "int32")
+SEMAPHORES = ["sD", "wld", "xld", "own", "ow2", "lp", "lh", "lo", "kp", "kf", "sO", "sP", "bp", "bps", "bo", "bos", "br", "brs",
+              "x1", "x1s", "x2", "x2s", "rw", "rws", "hs", "hss", "cw", "vs", "gs", "ss", "ps", "st", "ls"]
+
+TI = [(0, 0), (0, 4), (0, 8), (1, 4), (1, 8)]
+OUTER, THIRD, INNER, BOUND = (0, 7), (1, 6), (2, 5), (3, 4)
+OUTSIDE = {2: 6, 3: 7, 4: 0, 5: 1}
+X2_TO = {2: 4, 1: 5, 5: 3, 6: 2}
+
+
+def block(r):
+    return 256 * min(r, 7 - r)
+
+
+def pairs(r, t):
+    m = r // 2
+    d = (5 - t) // 2
+    return list(range(max(0, m - d), min(2, m + d - 1) + 1)) if t % 2 else list(range(max(0, m - d), min(3, m + d) + 1))
+
+
+def ranks(r, ts):
+    return sorted({2 * k + t % 2 + i for t in ts for k in pairs(r, t) for i in range(2)})
+
+
+def rank_program(g, core, T, topo):
+    S = T.sem
+    r = T.rank_of(core)
+
+    def dst(c):
+        a = topo.addr(c)
+        return DstId(rid=a[0], pnc=a[1])
+
+    def bits(es):
+        return sum(1 << e for e in es)
+
+    def sem(name, plane):
+        return S[name + ("s" if plane else "")]
+
+    def view(b, c, n, plane):
+        return T[b + "s"][:, c:c + n] if plane else T[b][:, c:c + n].bitcast(dt.uint8)
+
+    def helper(k):
+        c, to = T.cores[k], T.cores[OUTSIDE[k]]
+        return [x for x in topo.cores_of(c) if x not in T.cores and (topo.die(x) == topo.die(c)) == (k % 2 == 1)
+                and topo.may_write(x, to)][0]
+
+    if r is None:
+        for k in INNER + BOUND:
+            if core == helper(k):
+                to = sorted([OUTSIDE[k], OUTSIDE[k] ^ 1], key=lambda j: j in OUTER)
+                es = topo.engines(core, T.cores[to[0]])
+                n = len([e for e in topo.engines(T.cores[k], core) if e not in es])
+                for plane in (False, True):
+                    g.wait_ge(sem("hs", plane), n)
+                    g.remote_dma_fused([RemoteDMATransfer(
+                        dst_ids=[dst(T.cores[j]) for j in to], dma_engine_mask=bits(es), remote_sem=sem("rw", plane),
+                        srcs=[view("hw", 0, 256, plane)],
+                        dsts=[view("win", 1024 + 256 * (k % 2), 256, plane) for j in to])], local_sem=S.ls)
+                g.wait_ge(S.ls, 2 * len(es))
+        return
+
+    v, sc, sy, te = g.vector, g.scalar, g.sync, g.tensor
+    h = r // 4
+    bound, inner, third, outer = r in BOUND, r in INNER, r in THIRD, r in OUTER
+    mid = bound or inner
+    hand = inner or third
+    cv, cg, cs, cl, cst = [0], [0], [0], [0], [0]
+
+    def V(i):
+        i.then_inc(S.vs, 1)
+        cv[0] += 1
+        return cv[0]
+
+    def vw(n=None):
+        v.wait_ge(S.vs, n or cv[0])
+
+    def G(i):
+        i.then_inc(S.gs, 1)
+        cg[0] += 1
+        return cg[0]
+
+    def A(i):
+        i.then_inc(S.ss, 1)
+        cs[0] += 1
+        return cs[0]
+
+    def home_of_w(k, c):
+        return "hb" if k in INNER + THIRD or (k in BOUND and c >= 512) else "win"
+
+    partner = r ^ 1
+    far = [(2, 3), (0, 1), (7, 6), (5, 4)][r // 2]
+    land = [j for j in far if j in INNER + THIRD][0]
+    other = [k for k in range(8) if k // 4 != h]
+    near = topo.engines(core, T.cores[partner])
+    off = topo.engines(core, T.cores[land])
+    on = [e for e in near if e not in off]
+    non, noff, nall = len(on), len(off), len(near)
+    nx1 = noff if bound else nall
+
+    def home(j, s, hh):
+        return T["so" if j % 2 else "se"][0:8, s, hh, j // 2, :]
+
+    sy.dma_start(T.d3[0:64, :], T.dm[:, 0:12]).then_inc(S.sD, 16)
+    sc.dma_start(T.d3[64:128, :], T.dm[:, 8:20]).then_inc(S.sD, 16)
+    for hh in range(2):
+        for s, q in ((0, sy), (1, sc)):
+            q.dma_start(home(r, s, hh), T.dm[8 * s:8 * s + 8, 8 * hh:8 * hh + 12]).then_inc(S.ow2 if hh else S.own, 16)
+        if hh == 0:
+            sy.dma_start(T.wt[:], T.w[:]).then_inc(S.wld, 16)
+    sy.dma_start(T.xt[:], T.x[:]).then_inc(S.xld, 16)
+
+    G(g.iota(T.pi[:], [[0, 4]], 0, 1))
+    fl = dict(allow_small_or_imprecise_dtypes=True)
+    for s in range(2):
+        b = block(4 * h + s)
+        G(g.iota(T.li[:, 4 * s + 2 * h:4 * s + 2 * h + 2], [[block(4 * h + s + 2) - b, 2]], b, 32, **fl))
+        o = 4 * s + 2 * (1 - h)
+        if mid and (h == 0) == (s == 0):
+            k = [1024, 1280] if h == 0 else [1280, 1024]
+        elif mid:
+            k = [1280, 1280]
+        else:
+            k = [1024 + 256 * s] * 2
+        G(g.iota(T.li[:, o:o + 2], [[k[1] - k[0], 2]], k[0], 32, **fl))
+    if not outer:
+        G(g.iota(T.li[:, 8:9], [[1, 1]], 256 if bound else 512, 32, **fl))
+    nconst = cg[0]
+    V(v.memset(T.cr[:], 0.0))
+
+    g.wait_ge(S.sD, 32)
+    ld = T["ld%d" % r]
+
+    def lists(ks, e, sm):
+        return RemoteDMATransfer(dst_ids=[dst(T.cores[k]) for k in ks], dma_engine_mask=1 << e, remote_sem=sm,
+                                 srcs=[T.d3[:]], dsts=[ld[:] for k in ks])
+
+    g.remote_dma_fused([lists([partner], on[0], S.lp), lists(far, off[0], S.lh),
+                        lists([k for k in other if r in ranks(k, (0, 1, 2))], off[2], S.lo)], local_sem=S.ls)
+    cl[0] += 3
+
+    m, n2 = r // 2, 2 * h
+    o = T.so if r % 2 else T.se
+    v.wait_ge(S.own, 32)
+    vw()
+    V(v.tensor_tensor(T.cr[0:8, 0:1], o[0:8, 1, 0, m, m:m + 1], o[0:8, 0, 0, m, m:m + 1], Op.subtract))
+    if hand:
+        c = 4 + n2
+        V(v.tensor_tensor(T.cr[0:8, 1:2], o[0:8, 0, 0, m, c:c + 1], o[0:8, 1, 0, m, c:c + 1], Op.subtract))
+        V(v.tensor_tensor(T.cr[0:8, 2:3], o[0:8, 0, 0, m, c + 1:c + 2], o[0:8, 1, 0, m, c:c + 1], Op.subtract))
+        V(v.tensor_tensor(T.cr[0:8, 3:4], o[0:8, 1, 0, m, c + 1:c + 2], o[0:8, 0, 0, m, c + 1:c + 2], Op.subtract))
+    g.wait_ge(S.vs, cv[0])
+    n = 4 if hand else 1
+    to = [(land, off, S.kf, T["cx" if hand else "ck"])]
+    if not third:
+        to.append((partner, on, S.kp, T.cp))
+    g.remote_dma_fused([RemoteDMATransfer(dst_ids=[dst(T.cores[k])], dma_engine_mask=bits(es), remote_sem=sm,
+                                          srcs=[T.cr[:, 0:n]], dsts=[b[:, 0:n]]) for k, es, sm, b in to], local_sem=S.ls)
+    cl[0] += sum(len(x[1]) for x in to)
+
+    c0 = block(r)
+    v.wait_ge(S.wld, 16)
+    nq = V(v.quantize_mx(T.hb[:, c0:c0 + 256], T.hbs[:, c0:c0 + 256], T.wt[:]))
+    if outer:
+        V(v.quantize_mx(T.win[:, c0:c0 + 256], T.wins[:, c0:c0 + 256], T.wt[:]))
+    g.wait_ge(S.vs, nq)
+    for plane in (False, True):
+        g.remote_dma_fused([RemoteDMATransfer(dst_ids=[dst(T.cores[k])], dma_engine_mask=bits(es), remote_sem=sem(sm, plane),
+                                              srcs=[view("hb", c0, 256, plane)], dsts=[view(home_of_w(k, c0), c0, 256, plane)])
+                            for k, es, sm in ((partner, on, "bp"), (land, off, "bo"))], local_sem=S.ls)
+        cl[0] += non + noff
+
+    def put(c, sb, a, db, b, w, sm, plane, es):
+        ad = topo.addr(c)
+        g.remote_dma(view(db, b, w, plane), view(sb, a, w, plane), sem(sm, plane), S.ls, ad[1], ad[0], bits(es))
+        cl[0] += len(es)
+
+    if mid:
+        for plane in (False, True):
+            put(helper(r), "hb", c0, "hw", 0, 256, "hs", plane, on)
+
+    for b in ("sab", "dd", "ce", "co") + (() if outer else ("tt",)):
+        V(v.memset(T[b][:], 0.0))
+    v.wait_ge(S.gs, nconst)
+    V(v.tensor_scalar(T.pj[:], T.pi[:], 15, None, Op.bitwise_and))
+    V(v.tensor_scalar(T.p3[:], T.pi[:], 3, None, Op.bitwise_and))
+    if mid:
+        V(v.tensor_scalar(T.ph[:], T.pi[:], 14, None, Op.bitwise_and))
+    vw()
+    V(v.tensor_copy(T.pp[:, 0:1], T.pj[:, 0:1]))
+    V(v.tensor_scalar(T.pp[:, 1:2], T.pj[:, 0:1], 16.0, None, Op.add))
+    if mid:
+        V(v.tensor_scalar(T.pp[:, 2:3], T.pj[:, 0:1], -512.0, None, Op.add))
+        V(v.tensor_scalar(T.pp[:, 3:4], T.pj[:, 0:1], -496.0, None, Op.add))
+        V(v.tensor_scalar(T.pf[:, 0:1], T.ph[:, 0:1], 0.0 if h else 2.0, 4.0, Op.is_equal, Op.mult))
+        V(v.tensor_copy(T.oz[:], T.p3[:]))
+        vw()
+        V(v.tensor_scalar(T.oz[:, 0:1], T.p3[:, 0:1], T.pf[:, 0:1], None, Op.add))
+    V(v.tensor_copy(T.of[:], T.p3[:]))
+    for s in range(2):
+        V(v.tensor_copy(T.sab[0:8, s, 0:4], T.li[0:8, 4 * s:4 * s + 4]))
+
+    nx = [0]
+
+    def quantise_x():
+        v.wait_ge(S.xld, 16)
+        V(v.quantize_mx(T.xq[:, 0:512], T.xs[:, 0:512], T.xt[:, 0:2048]))
+        nx[0] = V(v.quantize_mx(T.xq[:, 512:640], T.xs[:, 512:640], T.xt[:, 2048:2560]))
+
+    if outer:
+        quantise_x()
+
+    cO, cP = [0], [0]
+    for s, q in ((0, sy), (1, sc)):
+        rest = []
+        for sm, js in ((S.lp, [partner]), (S.lh, list(far)), (S.lo, other)):
+            js = [j for j in js if j in ranks(r, (0, 1, 2))]
+            q.wait_ge(sm, len(js))
+            for j in js:
+                q.dma_start(home(j, s, 0), T["ld%d" % j][32 * s:32 * s + 32, :]).then_inc(S.sO, 16)
+                cO[0] += 16
+            rest += [j for j in js if j in ranks(r, (3, 4))]
+        for j in rest:
+            q.dma_start(home(j, s, 1), T["ld%d" % j][64 + 32 * s:96 + 32 * s, :]).then_inc(S.sP, 16)
+            cP[0] += 16
+
+    def chip_there(q, plane):
+        q.wait_ge(sem("bp", plane), non)
+
+    def half_there(q, plane):
+        chip_there(q, plane)
+        if hand:
+            q.wait_ge(sem("bo", plane), 2 * noff)
+        else:
+            q.wait_ge(sem("br", plane), non)
+
+    ncw = [0]
+
+    def to_win(a, n):
+        for plane in (False, True):
+            sy.dma_start(view("win", a, n, plane), view("hb", a, n, plane)).then_inc(S.cw, 16)
+            ncw[0] += 16
+
+    def pick(x, wa, wb, lt, nlist, buf, src, waits, w=256):
+        vw(nlist)
+        waits(v, False)
+        n1 = V(v.tensor_copy(T[buf][:, x:x + w].bitcast(dt.uint32), T[src][:, wa:wb].bitcast(dt.uint32).indirect(lt)))
+        sc.wait_ge(S.vs, nlist)
+        waits(sc, True)
+        return n1, A(sc.activation(T[buf + "s"][:, x:x + w], T[src + "s"][:, wa:wb].indirect(lt), Act.Copy))
+
+    stat = {}
+
+    if not outer:
+        W = T.wk
+        v.wait_ge(S.kp, non)
+        vw()
+        pa, pb = (T.cp[0:8, 0:1], T.cr[0:8, 0:1]) if r % 2 else (T.cr[0:8, 0:1], T.cp[0:8, 0:1])
+        if bound:
+            V(v.tensor_scalar(W[0:8, 2:3], pa, pb, -256.0, Op.is_gt, Op.mult))
+            vw()
+            V(v.tensor_scalar(T.tt[0:8, 0:1], W[0:8, 2:3], T.li[0:8, 8:9], None, Op.add))
+        else:
+            i = 4 + m - n2
+            ii = 4 if h else 5
+            V(v.tensor_tensor(W[0:8, i:i + 1], pa, pb, Op.is_gt))
+            v.wait_ge(S.kf, 2 * noff)
+            fa, fb = (T.cx[0:8, 0:1], T.ck[0:8, 0:1]) if min(far) in INNER + THIRD else (T.ck[0:8, 0:1], T.cx[0:8, 0:1])
+            V(v.tensor_tensor(W[0:8, 9 - i:10 - i], fa, fb, Op.is_gt))
+            fa, fb = (T.cr[0:8, 1:4], T.cx[0:8, 1:4]) if r % 2 else (T.cx[0:8, 1:4], T.cr[0:8, 1:4])
+            V(v.tensor_tensor(W[0:8, 8:11], fa, fb, Op.subtract))
+            vw()
+            V(v.tensor_tensor(W[0:8, 16:17], W[0:8, 4:5], W[0:8, 5:6], Op.add))
+            V(v.tensor_tensor(W[0:8, 14:15], W[0:8, 8:9], W[0:8, 4:5], Op.mult))
+            n = V(v.tensor_scalar(W[0:8, 15:16], W[0:8, 10:11], W[0:8, 5:6], W[0:8, 9:10], Op.mult, Op.add))
+            V(v.tensor_scalar(W[0:8, 18:19], W[0:8, ii:ii + 1], 256.0, T.li[0:8, 8:9], Op.mult, Op.add))
+            vw(n)
+            V(v.tensor_scalar(W[0:8, 17:18], W[0:8, 16:17], -256.0, -256.0, Op.mult, Op.add))
+            V(v.tensor_scalar(W[0:8, 20:21], W[0:8, 15:16], W[0:8, 14:15], None, Op.is_gt))
+            vw()
+            V(v.tensor_scalar(T.tt[0:8, 0:1], W[0:8, 20:21], W[0:8, 17:18], W[0:8, 18:19], Op.mult, Op.add))
+        vw()
+        n = V(v.transpose(T.tr[0:32, :], T.tt[0:32, :]))
+        g.wait_ge(S.vs, n)
+        n = G(g.partition_broadcast(T.bj[:], T.tr[0:1, 0:8], 128))
+        v.wait_ge(S.gs, n)
+        V(v.tensor_scalar(T.jl[:, 0:16:2], T.bj[:], T.pp[:, 0:1], None, Op.add))
+        njl = V(v.tensor_scalar(T.jl[:, 1:16:2], T.bj[:], T.pp[:, 1:2], None, Op.add))
+        if bound:
+            n1, n2_ = pick(0, 512, 1024, T.jl[:], njl, "pa", "hb", chip_there)
+            stat[0] = ("pa", 0, n1, n2_)
+            g.wait_ge(S.vs, n1)
+            put(T.cores[7 - r], "pa", 0, "win", 1024, 256, "x1", False, off)
+            g.wait_ge(S.ss, n2_)
+            put(T.cores[7 - r], "pa", 0, "win", 1024, 256, "x1", True, off)
+        quantise_x()
+
+    def send_x2():
+        x = 256 if inner else 768
+        n1, n2_ = pick(x, 0, 1024, T.jl[:], njl, "pa", "hb", half_there)
+        if inner:
+            stat[1] = ("pa", x, n1, n2_)
+        for plane, n in ((False, n1), (True, n2_)):
+            g.wait_ge(S.ss if plane else S.vs, n)
+            put(T.cores[X2_TO[r]], "pa", x, "win", 1280, 256, "x2", plane, off)
+
+    if hand:
+        fc = 0 if inner else 512
+        for plane in (False, True):
+            half_there(g, plane)
+            put(T.cores[partner], "hb", fc, "win", fc, 512, "br", plane, on)
+        if inner:
+            send_x2()
+
+    PR = [pairs(r, t) for t in range(5)]
+    COL, e = {}, 4
+    for t in (4, 3, 2, 1):
+        COL[t] = e
+        e += 4 * len(PR[t])
+    SIZE = [e, COL[1], COL[2], COL[3], 4]
+
+    def numbers(t):
+        hh, f = TI[t]
+        a, b = PR[t][0], PR[t][-1] + 1
+        to = T.sab[0:8, :, COL[t]:COL[t] + 4 * (b - a)] if t else T.e0[0:8, :, 0:4 * (b - a)]
+        if t % 2 == 0:
+            V(v.tensor_tensor(to, T.se[0:8, :, hh, a:b, f:f + 4], T.so[0:8, :, hh, a:b, f:f + 4], Op.subtract))
+        else:
+            V(v.tensor_tensor(to, T.so[0:8, :, hh, a:b, f:f + 4], T.se[0:8, :, hh, a + 1:b + 1, f:f + 4], Op.subtract))
+
+    level = [0] * 8
+    need = []
+    for t in range(5):
+        for k in range(t % 2, 7, 2):
+            level[k] = level[k + 1] = max(level[k], level[k + 1])
+        if t < 2:
+            level[(4 + t) if h == 0 else (3 - t)] = 1 + t
+        need.append(level[r])
+
+    def ready(t):
+        lv = need[t]
+        if hand and t == 0:
+            return "pa", "hb", 512 if inner else 0, 1024 if inner else 512, chip_there
+        if third and t < 3:
+            return "pa", "hb", 0, 1024, half_there
+        if outer and t < 2:
+            return "pk", "win", 0, 512, chip_there
+
+        def waits(q, plane):
+            if bound and t == 1:
+                chip_there(q, plane)
+            else:
+                half_there(q, plane)
+            if not outer:
+                q.wait_ge(S.cw, ncw[0])
+            if mid:
+                if lv >= 1:
+                    q.wait_ge(sem("x1", plane), nx1)
+                if lv >= 2:
+                    q.wait_ge(sem("x2", plane), noff)
+            elif lv:
+                q.wait_ge(sem("rw", plane), 2 * noff)
+        if bound and t == 1:
+            return "pk", "win", 512, 1280, waits
+        return "pk", "win", 0, 1024 + (256 * lv if mid else 512 * lv), waits
+
+    nlist = {}
+
+    def make_lists(t0, t1, k, shift=False):
+        v.wait_ge(S.gs, k)
+        fr = T.bf[:, 8 * t0:8 * t1]
+        o = 2 if shift else 0
+        V(v.tensor_scalar(T.lu[:, 16 * t0:16 * t1:2], fr, T.pp[:, o:o + 1], None, Op.add))
+        n = V(v.tensor_scalar(T.lu[:, 16 * t0 + 1:16 * t1:2], fr, T.pp[:, o + 1:o + 2], None, Op.add))
+        for t in range(t0, t1):
+            nlist[t] = n
+
+    def do_pick(t):
+        buf, src, wa, wb, waits = ready(t)
+        n1, n2_ = pick(256 * t, wa, wb, T.lu[:, 16 * t:16 * t + 16], nlist[t], buf, src, waits)
+        stat[t] = (buf, 256 * t, n1, n2_)
+
+    v.wait_ge(S.own, 32)
+    v.wait_ge(S.sO, cO[0])
+    for t in range(3):
+        numbers(t)
+    v.wait_ge(S.ow2, 32)
+    v.wait_ge(S.sP, cP[0])
+    for t in (3, 4):
+        numbers(t)
+
+    f0, f1 = (1, 2) if bound else (0, 1) if inner else (0, 2)
+    groups = {f1 - 1: (f0, f1), 3: (2, 4), 4: (4, 5)}
+    pb, last = {}, cv[0]
+
+    def turn(t):
+        if t < f0 or f1 <= t < 2:
+            return
+        k = V(v.transpose(T.tf[0:32, 8 * t:8 * t + 32], T.sab[0:32, r % 2, m:m + 32]))
+        if t in groups:
+            a, b = groups[t]
+            g.wait_ge(S.vs, k)
+            pb[t] = G(g.partition_broadcast(T.bf[0:128, 8 * a:8 * b], T.tf[0:1, 8 * a:8 * b], 128))
+            if bound and t < 4:
+                plane = t > 1
+                g.wait_ge(sem("x1", plane), noff)
+                put(T.cores[partner], "win", 1024, "win", 1024, 256, "x1", plane, near)
+
+    for t in range(5):
+        n, odd = SIZE[t], t % 2
+        n16 = -(-n // 16)
+        lo, np = PR[t][0], len(PR[t])
+        a, b = (T.sab[0:8, 1, 0:n], T.sab[0:8, 0, 1:n + 1]) if odd else (T.sab[0:8, 0, 0:n], T.sab[0:8, 1, 0:n])
+        eb, c = (T.sab, COL[t] + lo) if t else (T.e0, lo)
+        w = 5 * np - 4
+        ea, eb = eb[0:8, odd, c:c + w:5], eb[0:8, 1 - odd, c + odd:c + odd + w:5]
+        cc = T.co if odd else T.ce
+        vw(last)
+        V(v.tensor_tensor(cc[0:8, lo:lo + np], eb, ea, Op.is_gt))
+        k = V(v.tensor_tensor(T.dd[0:8, 0:n], b, a, Op.subtract))
+        if t:
+            turn(t - 1)
+        vw(k)
+        of = T.oz if mid and t == 0 else T.of
+        k = V(v.tensor_tensor(T.cd[:, 0:16 * n16], cc[:, 0:8].indirect(of[:, 0:n16]), T.dd[:, 0:16 * n16], Op.mult))
+        if t == 3:
+            make_lists(f0, f1, pb[f1 - 1], mid)
+        vw(k)
+        V(v.tensor_tensor(a, a, T.cd[0:8, 0:n], Op.add))
+        last = V(v.tensor_tensor(b, b, T.cd[0:8, 0:n], Op.subtract))
+        if t == 0 and not outer:
+            sy.wait_ge(S.vs, last if bound else nq)
+            for plane in (False, True):
+                (half_there if hand else chip_there)(sy, plane)
+            to_win(512 if bound else 0, 512 if bound else 1024)
+        if third and t == 2:
+            send_x2()
+        if t == 3 and not bound:
+            do_pick(0)
+    vw(last)
+    turn(4)
+
+    copied = {}
+    VB = (2, 3) if inner else (2,)
+
+    def out(t):
+        o = 256 * t
+        e = [512 * ((2 * t + k) % 8) for k in range(2)]
+        v.wait_ge(S.ps, 2 * t + 1)
+        n1 = V(v.tensor_copy(T.ys[:, o:o + 128], T.acc[:, e[0]:e[0] + 128]))
+        if t in VB:
+            v.wait_ge(S.ps, 2 * t + 2)
+            n1 = V(v.tensor_copy(T.ys[:, o + 128:o + 256], T.acc[:, e[1]:e[1] + 128]))
+            n2_ = 0
+        else:
+            sc.wait_ge(S.ps, 2 * t + 2)
+            n2_ = A(sc.activation(T.ys[:, o + 128:o + 256], T.acc[:, e[1]:e[1] + 128], Act.Copy))
+        copied[t] = (n1, n2_)
+        sy.wait_ge(S.vs, n1)
+        if t < 4:
+            if n2_:
+                sy.wait_ge(S.ss, n2_)
+            sy.dma_start(T.y[:, o:o + 256], T.ys[:, o:o + 256]).then_inc(S.st, 16)
+            cst[0] += 16
+        else:
+            sy.dma_start(T.y[:, o:o + 128], T.ys[:, o:o + 128]).then_inc(S.st, 16)
+            sc.wait_ge(S.ss, n2_)
+            sc.dma_start(T.y[:, o + 128:o + 256], T.ys[:, o + 128:o + 256]).then_inc(S.st, 16)
+            cst[0] += 32
+
+    def product(t, ks=(0, 1)):
+        buf, x, n1, n2_ = stat[t]
+        te.wait_ge(S.vs, max(n1, nx[0]))
+        te.wait_ge(S.ss, n2_)
+        if t == 4:
+            te.wait_ge(S.vs, copied[0][0])
+            te.wait_ge(S.ss, copied[0][1])
+        for k in ks:
+            e = 512 * ((2 * t + k) % 8)
+            c = x + 128 * k
+            te.matmul_mx(T.acc[:, e:e + 128], T[buf][:, c:c + 128], T[buf + "s"][:, c:c + 128],
+                         T.xq[:, 128 * t:128 * t + 128], T.xs[:, 128 * t:128 * t + 128], True, True).then_inc(S.ps, 1)
+
+    for t in range(5):
+        if inner and t == 2:
+            out(1)
+        if t in (2, 4):
+            make_lists(t, min(5, t + 2), pb[4 if t == 4 else 3])
+        if t not in stat and t < 4:
+            do_pick(t)
+        if t < 4:
+            product(t)
+        else:
+            buf, src, wa, wb, waits = ready(t)
+            for k in range(2):
+                n1, n2_ = pick(256 * t + 128 * k, wa, wb, T.lu[:, 16 * t + 8 * k:16 * t + 8 * k + 8], nlist[t], buf, src,
+                               waits, 128)
+                stat[t] = (buf, 256 * t, n1, n2_)
+                product(t, (k,))
+        if t > 0 and (t != 2 or not inner):
+            out(t - 1)
+    out(4)
+
+    for plane in (False, True):
+        half_there(v, plane)
+        for name, n in (("x1", nx1), ("x2", noff)) if mid else (("rw", 2 * noff),):
+            v.wait_ge(sem(name, plane), n)
+    vw()
+    sc.wait_ge(S.ss, cs[0])
+    te.wait_ge(S.ps, 10)
+    sy.wait_ge(S.st, cst[0])
+    g.wait_ge(S.gs, cg[0])
+    g.wait_ge(S.ls, cl[0])

@@ -3,56 +3,72 @@ from concourse.mybir import dt, AluOpType as Op, ActivationFunctionType as Act
 
 C8 = "float8_e4m3fn_x4"
 SCRATCH = {
-    "d3": ("dram", [128, 3], "int32"),
+    "la": ("dram", [8, 128, 2], "int32"),
+    "lb": ("dram", [2, 128, 2], "int32"),
     "wt": ("sbuf", [128, 1024], "bfloat16"),
     "xt": ("sbuf", [128, 2560], "bfloat16"),
     "xq": ("sbuf", [128, 640], C8), "xs": ("sbuf", [128, 640], "uint8"),
-    "hb": ("sbuf", [128, 1024], C8), "hbs": ("sbuf", [128, 1024], "uint8"),
-    "win": ("sbuf", [128, 1536], C8), "wins": ("sbuf", [128, 1536], "uint8"),
-    "pa": ("sbuf", [128, 1024], C8), "pas": ("sbuf", [128, 1024], "uint8"),
-    "hw": ("sbuf", [128, 256], C8), "hws": ("sbuf", [128, 256], "uint8"),
+    "wq": ("sbuf", [128, 512], C8), "wqs": ("sbuf", [128, 512], "uint8"),
+    "wa": ("sbuf", [128, 1280], C8), "was": ("sbuf", [128, 1280], "uint8"),
+    "wb": ("sbuf", [128, 1536], C8), "wbs": ("sbuf", [128, 1536], "uint8"),
+    "hw": ("sbuf", [128, 512], C8), "hws": ("sbuf", [128, 512], "uint8"),
+    "hx": ("sbuf", [128, 256], C8), "hxs": ("sbuf", [128, 256], "uint8"),
+    "px": ("sbuf", [128, 256], C8), "pxs": ("sbuf", [128, 256], "uint8"),
+    "pa": ("sbuf", [128, 256], C8), "pas": ("sbuf", [128, 256], "uint8"),
     "pk": ("sbuf", [128, 1280], C8), "pks": ("sbuf", [128, 1280], "uint8"),
-    "se": ("sbuf", [128, 2, 2, 4, 12], "int32"), "so": ("sbuf", [128, 2, 2, 4, 12], "int32"),
-    "cr": ("sbuf", [128, 4], "float32"),
-    "cp": ("sbuf", [128, 4], "float32"), "ck": ("sbuf", [128, 4], "float32"), "cx": ("sbuf", [128, 4], "float32"),
-    "sab": ("sbuf", [128, 2, 68], "float32"),
-    "e0": ("sbuf", [128, 2, 16], "float32"),
-    "dd": ("sbuf", [128, 64], "float32"), "cd": ("sbuf", [128, 64], "float32"),
+    "sl": ("sbuf", [128, 4, 16], "int32"), "sm": ("sbuf", [128, 16], "int32"),
+    "ea": ("sbuf", [128, 8], "int32"),
+    "eu": ("sbuf", [128, 64], "float32"),
+    "s0": ("sbuf", [128, 48], "float32"), "e0": ("sbuf", [128, 16], "float32"),
+    "sab": ("sbuf", [128, 2, 48], "float32"),
+    "dd": ("sbuf", [128, 48], "float32"), "cd": ("sbuf", [128, 48], "float32"),
     "ce": ("sbuf", [128, 8], "float32"), "co": ("sbuf", [128, 8], "float32"),
-    "wk": ("sbuf", [128, 32], "float32"),
-    "li": ("sbuf", [128, 12], "float32"), "pp": ("sbuf", [128, 4], "float32"),
+    "wk": ("sbuf", [128, 32], "float32"), "pp": ("sbuf", [128, 2], "float32"),
     "pi": ("sbuf", [128, 4], "int32"), "pj": ("sbuf", [128, 4], "int32"), "p3": ("sbuf", [128, 4], "int32"),
-    "ph": ("sbuf", [128, 4], "int32"), "pf": ("sbuf", [128, 2], "float32"),
-    "of": ("sbuf", [128, 4], "uint16"), "oz": ("sbuf", [128, 4], "uint16"),
-    "tt": ("sbuf", [128, 32], "float32"), "tr": ("sbuf", [128, 32], "float32"),
-    "bj": ("sbuf", [128, 8], "float32"), "jl": ("sbuf", [128, 16], "uint16"),
-    "tf": ("sbuf", [128, 64], "float32"), "bf": ("sbuf", [128, 40], "float32"), "lu": ("sbuf", [128, 80], "uint16"),
+    "of": ("sbuf", [128, 4], "uint16"),
+    "tf": ("sbuf", [128, 160], "float32"), "bf": ("sbuf", [128, 40], "float32"), "lu": ("sbuf", [128, 80], "uint16"),
     "ys": ("sbuf", [128, 1280], "float32"),
     "acc": ("psum", [128, 4096], "float32"),
 }
-for _j in range(8):
-    SCRATCH["ld%d" % _j] = ("dram", [128, 3], "int32")
-SEMAPHORES = ["sD", "wld", "xld", "own", "ow2", "lp", "lh", "lo", "kp", "kf", "sO", "sP", "bp", "bps", "bo", "bos", "br", "brs",
-              "x1", "x1s", "x2", "x2s", "rw", "rws", "hs", "hss", "cw", "vs", "gs", "ss", "ps", "st", "ls"]
+SEMAPHORES = ["sD", "sE", "sF", "ke", "wld", "xld", "l0", "l1", "l2", "l3", "lq", "li", "sO", "sP", "cw", "cws",
+              "bp", "bps", "bo", "bos", "br", "brs", "x1", "x1s", "x2", "x2s", "x3", "hs", "hss", "ht", "hts",
+              "vs", "gs", "ss", "ps", "st", "ls"]
 
-TI = [(0, 0), (0, 4), (0, 8), (1, 4), (1, 8)]
-OUTER, THIRD, INNER, BOUND = (0, 7), (1, 6), (2, 5), (3, 4)
-OUTSIDE = {2: 6, 3: 7, 4: 0, 5: 1}
-X2_TO = {2: 4, 1: 5, 5: 3, 6: 2}
+OUTER, THIRD, INNER, BOUND = 0, 1, 2, 3
+X1, X2 = 8, 9
 
 
-def block(r):
-    return 256 * min(r, 7 - r)
+def role(r):
+    return min(r, 7 - r)
+
+
+def of_role(h, k):
+    return 7 - k if h else k
+
+
+def land_of(k):
+    return of_role(k // 4, OUTER if role(k) >= INNER else INNER)
+
+
+def col(r, j):
+    k = role(r)
+    if j == X1:
+        return 512 if k == BOUND else 1024
+    if j == X2:
+        return 1280 if k >= INNER else 1024
+    if k < INNER:
+        return 256 * role(j)
+    return 256 * (j % 2) + (0 if j // 2 == r // 2 else 512 if k == INNER else 768)
+
+
+def win(r):
+    return "wa" if role(r) < INNER else "wb"
 
 
 def pairs(r, t):
     m = r // 2
     d = (5 - t) // 2
     return list(range(max(0, m - d), min(2, m + d - 1) + 1)) if t % 2 else list(range(max(0, m - d), min(3, m + d) + 1))
-
-
-def ranks(r, ts):
-    return sorted({2 * k + t % 2 + i for t in ts for k in pairs(r, t) for i in range(2)})
 
 
 def rank_program(g, core, T, topo):
@@ -73,30 +89,32 @@ def rank_program(g, core, T, topo):
         return T[b + "s"][:, c:c + n] if plane else T[b][:, c:c + n].bitcast(dt.uint8)
 
     def helper(k):
-        c, to = T.cores[k], T.cores[OUTSIDE[k]]
-        return [x for x in topo.cores_of(c) if x not in T.cores and (topo.die(x) == topo.die(c)) == (k % 2 == 1)
-                and topo.may_write(x, to)][0]
+        c = T.cores[k]
+        return [x for x in topo.cores_of(c) if topo.die(x) != topo.die(c) and topo.may_write(x, T.cores[land_of(k)])][0]
 
     if r is None:
-        for k in INNER + BOUND:
-            if core == helper(k):
-                to = sorted([OUTSIDE[k], OUTSIDE[k] ^ 1], key=lambda j: j in OUTER)
-                es = topo.engines(core, T.cores[to[0]])
-                n = len([e for e in topo.engines(T.cores[k], core) if e not in es])
-                for plane in (False, True):
-                    g.wait_ge(sem("hs", plane), n)
-                    g.remote_dma_fused([RemoteDMATransfer(
-                        dst_ids=[dst(T.cores[j]) for j in to], dma_engine_mask=bits(es), remote_sem=sem("rw", plane),
-                        srcs=[view("hw", 0, 256, plane)],
-                        dsts=[view("win", 1024 + 256 * (k % 2), 256, plane) for j in to])], local_sem=S.ls)
-                g.wait_ge(S.ls, 2 * len(es))
+        for k in range(8):
+            if role(k) in (OUTER, BOUND) and core == helper(k):
+                j, z = land_of(k), of_role(1 - k // 4, THIRD)
+                es = topo.engines(core, T.cores[j])
+                n = len(es)
+                jobs = [("hs", 2 * n, True, "hw", 0, 512, j, 512, "bo")]
+                if role(k) == OUTER:
+                    jobs.insert(0, ("hs", n, False, "hw", col(j, k) - 512, 256, j, col(j, k), "bo"))
+                else:
+                    jobs += [("ht", n, plane, "hx", 0, 256, z, col(z, X1), "x1") for plane in (False, True)]
+                for wait, cnt, plane, b, a, w, y, x, name in jobs:
+                    g.wait_ge(sem(wait, plane), cnt)
+                    ad = topo.addr(T.cores[y])
+                    g.remote_dma(view(win(y), x, w, plane), view(b, a, w, plane), sem(name, plane), S.ls, ad[1], ad[0], bits(es))
+                g.wait_ge(S.ls, n * len(jobs))
         return
 
     v, sc, sy, te = g.vector, g.scalar, g.sync, g.tensor
-    h = r // 4
-    bound, inner, third, outer = r in BOUND, r in INNER, r in THIRD, r in OUTER
-    mid = bound or inner
-    hand = inner or third
+    h, m, ro = r // 4, r // 2, role(r)
+    outer, third, inner, bound = ro == OUTER, ro == THIRD, ro == INNER, ro == BOUND
+    mid = inner or bound
+    W = win(r)
     cv, cg, cs, cl, cst = [0], [0], [0], [0], [0]
 
     def V(i):
@@ -117,393 +135,167 @@ def rank_program(g, core, T, topo):
         cs[0] += 1
         return cs[0]
 
-    def home_of_w(k, c):
-        return "hb" if k in INNER + THIRD or (k in BOUND and c >= 512) else "win"
-
-    partner = r ^ 1
-    far = [(2, 3), (0, 1), (7, 6), (5, 4)][r // 2]
-    land = [j for j in far if j in INNER + THIRD][0]
-    other = [k for k in range(8) if k // 4 != h]
+    partner, land = r ^ 1, land_of(r)
     near = topo.engines(core, T.cores[partner])
     off = topo.engines(core, T.cores[land])
     on = [e for e in near if e not in off]
     non, noff, nall = len(on), len(off), len(near)
-    nx1 = noff if bound else nall
+    PR = [pairs(r, t) for t in range(5)]
 
-    def home(j, s, hh):
-        return T["so" if j % 2 else "se"][0:8, s, hh, j // 2, :]
+    def send(plane, w, to):
+        g.remote_dma_fused([RemoteDMATransfer(dst_ids=[dst(c)], dma_engine_mask=bits(es), remote_sem=sem(sm, plane),
+                                              srcs=[view(a, x, w, plane)], dsts=[view(b, y, w, plane)])
+                            for c, es, sm, a, x, b, y in to], local_sem=S.ls)
+        cl[0] += sum(len(x[1]) for x in to)
 
-    sy.dma_start(T.d3[0:64, :], T.dm[:, 0:12]).then_inc(S.sD, 16)
-    sc.dma_start(T.d3[64:128, :], T.dm[:, 8:20]).then_inc(S.sD, 16)
-    for hh in range(2):
-        for s, q in ((0, sy), (1, sc)):
-            q.dma_start(home(r, s, hh), T.dm[8 * s:8 * s + 8, 8 * hh:8 * hh + 12]).then_inc(S.ow2 if hh else S.own, 16)
-        if hh == 0:
-            sy.dma_start(T.wt[:], T.w[:]).then_inc(S.wld, 16)
+    u = 4 * (r % 2)
+    sy.dma_start(T.la[r], T.dm[:, 0:16]).then_inc(S.sD, 16)
+    sc.dma_start(T.ea[0:64, u:u + 2], T.dm[:, m:m + 8]).then_inc(S.sF, 16)
+    sc.dma_start(T.lb[r % 2], T.dm[:, 4:20]).then_inc(S.sE, 16)
+    sy.dma_start(T.wt[:], T.w[:]).then_inc(S.wld, 16)
     sy.dma_start(T.xt[:], T.x[:]).then_inc(S.xld, 16)
 
+    def first(j):
+        return col(r, j if j // 4 == h else X1 if role(j) == BOUND else X2)
+
     G(g.iota(T.pi[:], [[0, 4]], 0, 1))
-    fl = dict(allow_small_or_imprecise_dtypes=True)
     for s in range(2):
-        b = block(4 * h + s)
-        G(g.iota(T.li[:, 4 * s + 2 * h:4 * s + 2 * h + 2], [[block(4 * h + s + 2) - b, 2]], b, 32, **fl))
-        o = 4 * s + 2 * (1 - h)
-        if mid and (h == 0) == (s == 0):
-            k = [1024, 1280] if h == 0 else [1280, 1024]
-        elif mid:
-            k = [1280, 1280]
-        else:
-            k = [1024 + 256 * s] * 2
-        G(g.iota(T.li[:, o:o + 2], [[k[1] - k[0], 2]], k[0], 32, **fl))
-    if not outer:
-        G(g.iota(T.li[:, 8:9], [[1, 1]], 256 if bound else 512, 32, **fl))
+        if s:
+            g.wait_ge(S.gs, cg[0])
+        for k in (0, 2):
+            a, b = first(2 * k + s), first(2 * k + 2 + s)
+            G(g.iota(T.s0[32 * s:32 * s + 32, k:k + 2], [[b - a, 2]], a, 8, allow_small_or_imprecise_dtypes=True))
     nconst = cg[0]
-    V(v.memset(T.cr[:], 0.0))
-
-    g.wait_ge(S.sD, 32)
-    ld = T["ld%d" % r]
-
-    def lists(ks, e, sm):
-        return RemoteDMATransfer(dst_ids=[dst(T.cores[k]) for k in ks], dma_engine_mask=1 << e, remote_sem=sm,
-                                 srcs=[T.d3[:]], dsts=[ld[:] for k in ks])
-
-    g.remote_dma_fused([lists([partner], on[0], S.lp), lists(far, off[0], S.lh),
-                        lists([k for k in other if r in ranks(k, (0, 1, 2))], off[2], S.lo)], local_sem=S.ls)
-    cl[0] += 3
-
-    m, n2 = r // 2, 2 * h
-    o = T.so if r % 2 else T.se
-    v.wait_ge(S.own, 32)
-    vw()
-    V(v.tensor_tensor(T.cr[0:8, 0:1], o[0:8, 1, 0, m, m:m + 1], o[0:8, 0, 0, m, m:m + 1], Op.subtract))
-    if hand:
-        c = 4 + n2
-        V(v.tensor_tensor(T.cr[0:8, 1:2], o[0:8, 0, 0, m, c:c + 1], o[0:8, 1, 0, m, c:c + 1], Op.subtract))
-        V(v.tensor_tensor(T.cr[0:8, 2:3], o[0:8, 0, 0, m, c + 1:c + 2], o[0:8, 1, 0, m, c:c + 1], Op.subtract))
-        V(v.tensor_tensor(T.cr[0:8, 3:4], o[0:8, 1, 0, m, c + 1:c + 2], o[0:8, 0, 0, m, c + 1:c + 2], Op.subtract))
-    g.wait_ge(S.vs, cv[0])
-    n = 4 if hand else 1
-    to = [(land, off, S.kf, T["cx" if hand else "ck"])]
-    if not third:
-        to.append((partner, on, S.kp, T.cp))
-    g.remote_dma_fused([RemoteDMATransfer(dst_ids=[dst(T.cores[k])], dma_engine_mask=bits(es), remote_sem=sm,
-                                          srcs=[T.cr[:, 0:n]], dsts=[b[:, 0:n]]) for k, es, sm, b in to], local_sem=S.ls)
-    cl[0] += sum(len(x[1]) for x in to)
-
-    c0 = block(r)
-    v.wait_ge(S.wld, 16)
-    nq = V(v.quantize_mx(T.hb[:, c0:c0 + 256], T.hbs[:, c0:c0 + 256], T.wt[:]))
-    if outer:
-        V(v.quantize_mx(T.win[:, c0:c0 + 256], T.wins[:, c0:c0 + 256], T.wt[:]))
-    g.wait_ge(S.vs, nq)
-    for plane in (False, True):
-        g.remote_dma_fused([RemoteDMATransfer(dst_ids=[dst(T.cores[k])], dma_engine_mask=bits(es), remote_sem=sem(sm, plane),
-                                              srcs=[view("hb", c0, 256, plane)], dsts=[view(home_of_w(k, c0), c0, 256, plane)])
-                            for k, es, sm in ((partner, on, "bp"), (land, off, "bo"))], local_sem=S.ls)
-        cl[0] += non + noff
-
-    def put(c, sb, a, db, b, w, sm, plane, es):
-        ad = topo.addr(c)
-        g.remote_dma(view(db, b, w, plane), view(sb, a, w, plane), sem(sm, plane), S.ls, ad[1], ad[0], bits(es))
-        cl[0] += len(es)
-
-    if mid:
-        for plane in (False, True):
-            put(helper(r), "hb", c0, "hw", 0, 256, "hs", plane, on)
-
-    for b in ("sab", "dd", "ce", "co") + (() if outer else ("tt",)):
+    ne = V(v.memset(T.ea[64:128, u:u + 4], 0))
+    V(v.memset(T.sl[:], 0))
+    nz = V(v.memset(T.sm[:], 0))
+    for b in ("sab", "ce", "co", "wk", "eu"):
         V(v.memset(T[b][:], 0.0))
+    V(v.memset(T.dd[:, 4:48], 0.0))
+    for k in range(4):
+        V(v.memset(T.dd[:, k:k + 1], float(first(2 * k + 1) - first(2 * k)) if k // 2 == h else 0.0))
     v.wait_ge(S.gs, nconst)
     V(v.tensor_scalar(T.pj[:], T.pi[:], 15, None, Op.bitwise_and))
     V(v.tensor_scalar(T.p3[:], T.pi[:], 3, None, Op.bitwise_and))
-    if mid:
-        V(v.tensor_scalar(T.ph[:], T.pi[:], 14, None, Op.bitwise_and))
     vw()
     V(v.tensor_copy(T.pp[:, 0:1], T.pj[:, 0:1]))
     V(v.tensor_scalar(T.pp[:, 1:2], T.pj[:, 0:1], 16.0, None, Op.add))
-    if mid:
-        V(v.tensor_scalar(T.pp[:, 2:3], T.pj[:, 0:1], -512.0, None, Op.add))
-        V(v.tensor_scalar(T.pp[:, 3:4], T.pj[:, 0:1], -496.0, None, Op.add))
-        V(v.tensor_scalar(T.pf[:, 0:1], T.ph[:, 0:1], 0.0 if h else 2.0, 4.0, Op.is_equal, Op.mult))
-        V(v.tensor_copy(T.oz[:], T.p3[:]))
-        vw()
-        V(v.tensor_scalar(T.oz[:, 0:1], T.p3[:, 0:1], T.pf[:, 0:1], None, Op.add))
     V(v.tensor_copy(T.of[:], T.p3[:]))
-    for s in range(2):
-        V(v.tensor_copy(T.sab[0:8, s, 0:4], T.li[0:8, 4 * s:4 * s + 4]))
+    V(v.tensor_copy(T.eu[0:32, 2:3], T.s0[32 * (r % 2):32 * (r % 2) + 32, m:m + 1]))
 
-    nx = [0]
+    def lists(ks, es, sm, b):
+        cl[0] += len(es)
+        return RemoteDMATransfer(dst_ids=[dst(T.cores[k]) for k in ks], dma_engine_mask=bits(es), remote_sem=sm,
+                                 srcs=[b], dsts=[b for k in ks])
 
-    def quantise_x():
-        v.wait_ge(S.xld, 16)
-        V(v.quantize_mx(T.xq[:, 0:512], T.xs[:, 0:512], T.xt[:, 0:2048]))
-        nx[0] = V(v.quantize_mx(T.xq[:, 512:640], T.xs[:, 512:640], T.xt[:, 2048:2560]))
+    for sm in (S.sD, S.sE, S.sF):
+        g.wait_ge(sm, 16)
+    g.wait_ge(S.vs, ne)
+    lsem = S["l%d" % m]
+    far = [k for k in range(8) if k // 4 == h and k // 2 != m]
+    to = [k for k in range(8) if k != r and m in pairs(k, 0)]
+    g.remote_dma_fused([lists([k], [e], lsem, T.la[r]) for k, e in zip(to, off)]
+                       + [lists([partner], off[-1:], S.lq, T.lb[r % 2]), lists([partner], on[0:4], S.ke, T.ea[:, u:u + 2])],
+                       local_sem=S.ls)
 
-    if outer:
-        quantise_x()
-
-    cO, cP = [0], [0]
-    for s, q in ((0, sy), (1, sc)):
-        rest = []
-        for sm, js in ((S.lp, [partner]), (S.lh, list(far)), (S.lo, other)):
-            js = [j for j in js if j in ranks(r, (0, 1, 2))]
-            q.wait_ge(sm, len(js))
-            for j in js:
-                q.dma_start(home(j, s, 0), T["ld%d" % j][32 * s:32 * s + 32, :]).then_inc(S.sO, 16)
-                cO[0] += 16
-            rest += [j for j in js if j in ranks(r, (3, 4))]
-        for j in rest:
-            q.dma_start(home(j, s, 1), T["ld%d" % j][64 + 32 * s:96 + 32 * s, :]).then_inc(S.sP, 16)
-            cP[0] += 16
-
-    def chip_there(q, plane):
-        q.wait_ge(sem("bp", plane), non)
-
-    def half_there(q, plane):
-        chip_there(q, plane)
-        if hand:
-            q.wait_ge(sem("bo", plane), 2 * noff)
+    c0, cp, cz = col(r, r), col(r, partner), col(land, r)
+    src = "wq" if mid else W
+    v.wait_ge(S.wld, 16)
+    nq = V(v.quantize_mx(T[src][:, c0:c0 + 256], T[src + "s"][:, c0:c0 + 256], T.wt[:]))
+    if mid:
+        V(v.quantize_mx(T.wb[:, c0:c0 + 256], T.wbs[:, c0:c0 + 256], T.wt[:]))
+    g.wait_ge(S.vs, nq)
+    for plane in (False, True):
+        to = [(T.cores[partner], on[4 * i:4 * i + 4], "bp", src, c0 + 128 * i, "wq" if inner else W, c0 + 128 * i)
+              for i in range(2)]
+        if outer or plane:
+            to += [(helper(r), off[4 * i:4 * i + 4], "hs", src, c0 + 128 * i, "hw", cz - 512 + 128 * i) for i in range(2)]
         else:
-            q.wait_ge(sem("br", plane), non)
-
-    ncw = [0]
-
-    def to_win(a, n):
-        for plane in (False, True):
-            sy.dma_start(view("win", a, n, plane), view("hb", a, n, plane)).then_inc(S.cw, 16)
-            ncw[0] += 16
-
-    def pick(x, wa, wb, lt, nlist, buf, src, waits, w=256):
-        vw(nlist)
-        waits(v, False)
-        n1 = V(v.tensor_copy(T[buf][:, x:x + w].bitcast(dt.uint32), T[src][:, wa:wb].bitcast(dt.uint32).indirect(lt)))
-        sc.wait_ge(S.vs, nlist)
-        waits(sc, True)
-        return n1, A(sc.activation(T[buf + "s"][:, x:x + w], T[src + "s"][:, wa:wb].indirect(lt), Act.Copy))
-
-    stat = {}
-
+            to += [(T.cores[land], off, "bo", src, c0, win(land), cz)]
+        send(plane, 128, to)
     if not outer:
-        W = T.wk
-        v.wait_ge(S.kp, non)
-        vw()
-        pa, pb = (T.cp[0:8, 0:1], T.cr[0:8, 0:1]) if r % 2 else (T.cr[0:8, 0:1], T.cp[0:8, 0:1])
-        if bound:
-            V(v.tensor_scalar(W[0:8, 2:3], pa, pb, -256.0, Op.is_gt, Op.mult))
-            vw()
-            V(v.tensor_scalar(T.tt[0:8, 0:1], W[0:8, 2:3], T.li[0:8, 8:9], None, Op.add))
-        else:
-            i = 4 + m - n2
-            ii = 4 if h else 5
-            V(v.tensor_tensor(W[0:8, i:i + 1], pa, pb, Op.is_gt))
-            v.wait_ge(S.kf, 2 * noff)
-            fa, fb = (T.cx[0:8, 0:1], T.ck[0:8, 0:1]) if min(far) in INNER + THIRD else (T.ck[0:8, 0:1], T.cx[0:8, 0:1])
-            V(v.tensor_tensor(W[0:8, 9 - i:10 - i], fa, fb, Op.is_gt))
-            fa, fb = (T.cr[0:8, 1:4], T.cx[0:8, 1:4]) if r % 2 else (T.cx[0:8, 1:4], T.cr[0:8, 1:4])
-            V(v.tensor_tensor(W[0:8, 8:11], fa, fb, Op.subtract))
-            vw()
-            V(v.tensor_tensor(W[0:8, 16:17], W[0:8, 4:5], W[0:8, 5:6], Op.add))
-            V(v.tensor_tensor(W[0:8, 14:15], W[0:8, 8:9], W[0:8, 4:5], Op.mult))
-            n = V(v.tensor_scalar(W[0:8, 15:16], W[0:8, 10:11], W[0:8, 5:6], W[0:8, 9:10], Op.mult, Op.add))
-            V(v.tensor_scalar(W[0:8, 18:19], W[0:8, ii:ii + 1], 256.0, T.li[0:8, 8:9], Op.mult, Op.add))
-            vw(n)
-            V(v.tensor_scalar(W[0:8, 17:18], W[0:8, 16:17], -256.0, -256.0, Op.mult, Op.add))
-            V(v.tensor_scalar(W[0:8, 20:21], W[0:8, 15:16], W[0:8, 14:15], None, Op.is_gt))
-            vw()
-            V(v.tensor_scalar(T.tt[0:8, 0:1], W[0:8, 20:21], W[0:8, 17:18], W[0:8, 18:19], Op.mult, Op.add))
-        vw()
-        n = V(v.transpose(T.tr[0:32, :], T.tt[0:32, :]))
-        g.wait_ge(S.vs, n)
-        n = G(g.partition_broadcast(T.bj[:], T.tr[0:1, 0:8], 128))
-        v.wait_ge(S.gs, n)
-        V(v.tensor_scalar(T.jl[:, 0:16:2], T.bj[:], T.pp[:, 0:1], None, Op.add))
-        njl = V(v.tensor_scalar(T.jl[:, 1:16:2], T.bj[:], T.pp[:, 1:2], None, Op.add))
-        if bound:
-            n1, n2_ = pick(0, 512, 1024, T.jl[:], njl, "pa", "hb", chip_there)
-            stat[0] = ("pa", 0, n1, n2_)
-            g.wait_ge(S.vs, n1)
-            put(T.cores[7 - r], "pa", 0, "win", 1024, 256, "x1", False, off)
-            g.wait_ge(S.ss, n2_)
-            put(T.cores[7 - r], "pa", 0, "win", 1024, 256, "x1", True, off)
-        quantise_x()
+        g.wait_ge(S.li, 2)
+        send(False, 128, [(T.cores[land], off, "bo", src, c0 + 128, win(land), cz + 128)])
 
-    def send_x2():
-        x = 256 if inner else 768
-        n1, n2_ = pick(x, 0, 1024, T.jl[:], njl, "pa", "hb", half_there)
-        if inner:
-            stat[1] = ("pa", x, n1, n2_)
-        for plane, n in ((False, n1), (True, n2_)):
-            g.wait_ge(S.ss if plane else S.vs, n)
-            put(T.cores[X2_TO[r]], "pa", x, "win", 1280, 256, "x2", plane, off)
+    v.wait_ge(S.xld, 16)
+    V(v.quantize_mx(T.xq[:, 0:512], T.xs[:, 0:512], T.xt[:, 0:2048]))
+    nx = V(v.quantize_mx(T.xq[:, 512:640], T.xs[:, 512:640], T.xt[:, 2048:2560]))
 
-    if hand:
-        fc = 0 if inner else 512
+    chips = sorted(PR[0], key=lambda k: (k != m, k // 2 != h))
+    for q in (sy, sc):
+        q.wait_ge(S.vs, nz)
+    sy.wait_ge(S.sD, 16)
+    sc.wait_ge(S.sE, 16)
+    sc.wait_ge(S.lq, 1)
+    sc.dma_start(T.sm[0:128:4, :], T.lb[:]).then_inc(S.sP, 16)
+    for i, k in enumerate(chips):
+        q = (sy, sy, sc, sy)[i]
+        q.wait_ge(S["l%d" % k], 1 if k == m else 2)
+        q.dma_start(T.sl[0:128:4, k, :], T.la[2 * k:2 * k + 2]).then_inc(S.sO, 16)
+    if not outer:
+        sy.sem_inc(S.li, 1)
+        sc.sem_inc(S.li, 1)
+    if bound:
         for plane in (False, True):
-            half_there(g, plane)
-            put(T.cores[partner], "hb", fc, "win", fc, 512, "br", plane, on)
-        if inner:
-            send_x2()
+            sy.wait_ge(sem("bp", plane), non)
+            sy.dma_start(view("wb", cp, 256, plane), view("wq", cp, 256, plane)).then_inc(sem("cw", plane), 16)
 
-    PR = [pairs(r, t) for t in range(5)]
-    COL, e = {}, 4
-    for t in (4, 3, 2, 1):
-        COL[t] = e
-        e += 4 * len(PR[t])
-    SIZE = [e, COL[1], COL[2], COL[3], 4]
+    nbo = [4 * noff if outer else 3 * noff, noff]
+    parts = [[(512, "bp", non), (1024, "bo", 0), (1280, "x1", nall)],
+             [(512, "bp", non), (1024, "br", non), (1280, "x1", noff)],
+             [(512, "bp", non), (1024, "bo", 0), (1280, "x1", nall), (1408, "x2", nall), (1536, "x3", noff)],
+             [(512, "bp", non), (768, "cw", 16), (768, "x1", noff), (1280, "br", non), (1408, "x2", noff),
+              (1536, "x3", noff)]][ro]
+    want = [[(0, r, 512), (1, land, 1024), (2, r, 1024), (4, r, 1280)],
+            [(0, r, 512), (1, r, 1024), (2, r, 1024), (3, r, 1280), (4, r, 1280)],
+            [(0, r, 512), (1, r, 1024), (2, r, 1280), (3, r, 1280), (4, r, 1536)],
+            [(0, r, 512), (1, r, 768), (2, r, 1280), (3, r, 1536), (4, r, 1536)]][ro]
+    groups = {0: (0, 1), 1: (1, 2), 4: (2, 4)} if outer else {0: (0, 1), 3: (1, 4), 4: (4, 5)}
+    seen = {}
 
-    def numbers(t):
-        hh, f = TI[t]
-        a, b = PR[t][0], PR[t][-1] + 1
-        to = T.sab[0:8, :, COL[t]:COL[t] + 4 * (b - a)] if t else T.e0[0:8, :, 0:4 * (b - a)]
-        if t % 2 == 0:
-            V(v.tensor_tensor(to, T.se[0:8, :, hh, a:b, f:f + 4], T.so[0:8, :, hh, a:b, f:f + 4], Op.subtract))
-        else:
-            V(v.tensor_tensor(to, T.so[0:8, :, hh, a:b, f:f + 4], T.se[0:8, :, hh, a + 1:b + 1, f:f + 4], Op.subtract))
+    def there(q, end, plane):
+        for e, name, n in parts:
+            if e <= end and (name, plane) not in seen and (name, plane) != ("x3", True):
+                q.wait_ge(sem(name, plane), n or nbo[plane])
+                seen[(name, plane)] = 1
 
-    level = [0] * 8
-    need = []
-    for t in range(5):
-        for k in range(t % 2, 7, 2):
-            level[k] = level[k + 1] = max(level[k], level[k + 1])
-        if t < 2:
-            level[(4 + t) if h == 0 else (3 - t)] = 1 + t
-        need.append(level[r])
+    nlist, pb, stat, copied = {}, {}, {}, {}
 
-    def ready(t):
-        lv = need[t]
-        if hand and t == 0:
-            return "pa", "hb", 512 if inner else 0, 1024 if inner else 512, chip_there
-        if third and t < 3:
-            return "pa", "hb", 0, 1024, half_there
-        if outer and t < 2:
-            return "pk", "win", 0, 512, chip_there
-
-        def waits(q, plane):
-            if bound and t == 1:
-                chip_there(q, plane)
-            else:
-                half_there(q, plane)
-            if not outer:
-                q.wait_ge(S.cw, ncw[0])
-            if mid:
-                if lv >= 1:
-                    q.wait_ge(sem("x1", plane), nx1)
-                if lv >= 2:
-                    q.wait_ge(sem("x2", plane), noff)
-            elif lv:
-                q.wait_ge(sem("rw", plane), 2 * noff)
-        if bound and t == 1:
-            return "pk", "win", 512, 1280, waits
-        return "pk", "win", 0, 1024 + (256 * lv if mid else 512 * lv), waits
-
-    nlist = {}
-
-    def make_lists(t0, t1, k, shift=False):
-        v.wait_ge(S.gs, k)
-        fr = T.bf[:, 8 * t0:8 * t1]
-        o = 2 if shift else 0
-        V(v.tensor_scalar(T.lu[:, 16 * t0:16 * t1:2], fr, T.pp[:, o:o + 1], None, Op.add))
-        n = V(v.tensor_scalar(T.lu[:, 16 * t0 + 1:16 * t1:2], fr, T.pp[:, o + 1:o + 2], None, Op.add))
-        for t in range(t0, t1):
-            nlist[t] = n
-
-    def do_pick(t):
-        buf, src, wa, wb, waits = ready(t)
-        n1, n2_ = pick(256 * t, wa, wb, T.lu[:, 16 * t:16 * t + 16], nlist[t], buf, src, waits)
-        stat[t] = (buf, 256 * t, n1, n2_)
-
-    v.wait_ge(S.own, 32)
-    v.wait_ge(S.sO, cO[0])
-    for t in range(3):
-        numbers(t)
-    v.wait_ge(S.ow2, 32)
-    v.wait_ge(S.sP, cP[0])
-    for t in (3, 4):
-        numbers(t)
-
-    f0, f1 = (1, 2) if bound else (0, 1) if inner else (0, 2)
-    groups = {f1 - 1: (f0, f1), 3: (2, 4), 4: (4, 5)}
-    pb, last = {}, cv[0]
+    def pick(i, buf, x, a=0, b=16, fr=W):
+        end, lt, w = want[i][2], T.lu[:, 16 * i + a:16 * i + b], 16 * (b - a)
+        x += 16 * a
+        if end == 1536 and b == 8:
+            end -= 128
+        vw(nlist[i])
+        there(v, end, False)
+        n1 = V(v.tensor_copy(T[buf][:, x:x + w].bitcast(dt.uint32), T[fr][:, 0:end].bitcast(dt.uint32).indirect(lt)))
+        sc.wait_ge(S.vs, nlist[i])
+        there(sc, end, True)
+        return n1, A(sc.activation(T[buf + "s"][:, x:x + w], T[fr + "s"][:, 0:end].indirect(lt), Act.Copy))
 
     def turn(t):
-        if t < f0 or f1 <= t < 2:
-            return
-        k = V(v.transpose(T.tf[0:32, 8 * t:8 * t + 32], T.sab[0:32, r % 2, m:m + 32]))
+        for i, (z, j, _e) in enumerate(want):
+            if z == t:
+                fr = T.wk[0:32, :] if t == 4 else T.sab[0:32, j % 2, j // 2:j // 2 + 32] if t else T.eu[0:32, 32:64]
+                k = V(v.transpose(T.tf[0:32, 32 * i:32 * i + 32], fr))
         if t in groups:
             a, b = groups[t]
             g.wait_ge(S.vs, k)
-            pb[t] = G(g.partition_broadcast(T.bf[0:128, 8 * a:8 * b], T.tf[0:1, 8 * a:8 * b], 128))
-            if bound and t < 4:
-                plane = t > 1
-                g.wait_ge(sem("x1", plane), noff)
-                put(T.cores[partner], "win", 1024, "win", 1024, 256, "x1", plane, near)
+            pb[t] = G(g.partition_broadcast(T.bf[0:128, 8 * a:8 * b], T.tf[0:1, 32 * a:32 * b:4], 128))
 
-    for t in range(5):
-        n, odd = SIZE[t], t % 2
-        n16 = -(-n // 16)
-        lo, np = PR[t][0], len(PR[t])
-        a, b = (T.sab[0:8, 1, 0:n], T.sab[0:8, 0, 1:n + 1]) if odd else (T.sab[0:8, 0, 0:n], T.sab[0:8, 1, 0:n])
-        eb, c = (T.sab, COL[t] + lo) if t else (T.e0, lo)
-        w = 5 * np - 4
-        ea, eb = eb[0:8, odd, c:c + w:5], eb[0:8, 1 - odd, c + odd:c + odd + w:5]
-        cc = T.co if odd else T.ce
-        vw(last)
-        V(v.tensor_tensor(cc[0:8, lo:lo + np], eb, ea, Op.is_gt))
-        k = V(v.tensor_tensor(T.dd[0:8, 0:n], b, a, Op.subtract))
-        if t:
-            turn(t - 1)
-        vw(k)
-        of = T.oz if mid and t == 0 else T.of
-        k = V(v.tensor_tensor(T.cd[:, 0:16 * n16], cc[:, 0:8].indirect(of[:, 0:n16]), T.dd[:, 0:16 * n16], Op.mult))
-        if t == 3:
-            make_lists(f0, f1, pb[f1 - 1], mid)
-        vw(k)
-        V(v.tensor_tensor(a, a, T.cd[0:8, 0:n], Op.add))
-        last = V(v.tensor_tensor(b, b, T.cd[0:8, 0:n], Op.subtract))
-        if t == 0 and not outer:
-            sy.wait_ge(S.vs, last if bound else nq)
-            for plane in (False, True):
-                (half_there if hand else chip_there)(sy, plane)
-            to_win(512 if bound else 0, 512 if bound else 1024)
-        if third and t == 2:
-            send_x2()
-        if t == 3 and not bound:
-            do_pick(0)
-    vw(last)
-    turn(4)
-
-    copied = {}
-    VB = (2, 3) if inner else (2,)
-
-    def out(t):
-        o = 256 * t
-        e = [512 * ((2 * t + k) % 8) for k in range(2)]
-        v.wait_ge(S.ps, 2 * t + 1)
-        n1 = V(v.tensor_copy(T.ys[:, o:o + 128], T.acc[:, e[0]:e[0] + 128]))
-        if t in VB:
-            v.wait_ge(S.ps, 2 * t + 2)
-            n1 = V(v.tensor_copy(T.ys[:, o + 128:o + 256], T.acc[:, e[1]:e[1] + 128]))
-            n2_ = 0
-        else:
-            sc.wait_ge(S.ps, 2 * t + 2)
-            n2_ = A(sc.activation(T.ys[:, o + 128:o + 256], T.acc[:, e[1]:e[1] + 128], Act.Copy))
-        copied[t] = (n1, n2_)
-        sy.wait_ge(S.vs, n1)
-        if t < 4:
-            if n2_:
-                sy.wait_ge(S.ss, n2_)
-            sy.dma_start(T.y[:, o:o + 256], T.ys[:, o:o + 256]).then_inc(S.st, 16)
-            cst[0] += 16
-        else:
-            sy.dma_start(T.y[:, o:o + 128], T.ys[:, o:o + 128]).then_inc(S.st, 16)
-            sc.wait_ge(S.ss, n2_)
-            sc.dma_start(T.y[:, o + 128:o + 256], T.ys[:, o + 128:o + 256]).then_inc(S.st, 16)
-            cst[0] += 32
+    def make_lists(t):
+        a, b = groups[t]
+        v.wait_ge(S.gs, pb[t])
+        fr = T.bf[:, 8 * a:8 * b]
+        V(v.tensor_scalar(T.lu[:, 16 * a:16 * b:2], fr, T.pp[:, 0:1], None, Op.add))
+        n = V(v.tensor_scalar(T.lu[:, 16 * a + 1:16 * b:2], fr, T.pp[:, 1:2], None, Op.add))
+        for i in range(a, b):
+            nlist[i] = n
 
     def product(t, ks=(0, 1)):
-        buf, x, n1, n2_ = stat[t]
-        te.wait_ge(S.vs, max(n1, nx[0]))
-        te.wait_ge(S.ss, n2_)
+        buf, x, n1, n2 = stat[t]
+        te.wait_ge(S.vs, max(n1, nx))
+        te.wait_ge(S.ss, n2)
         if t == 4:
             te.wait_ge(S.vs, copied[0][0])
             te.wait_ge(S.ss, copied[0][1])
@@ -513,30 +305,176 @@ def rank_program(g, core, T, topo):
             te.matmul_mx(T.acc[:, e:e + 128], T[buf][:, c:c + 128], T[buf + "s"][:, c:c + 128],
                          T.xq[:, 128 * t:128 * t + 128], T.xs[:, 128 * t:128 * t + 128], True, True).then_inc(S.ps, 1)
 
-    for t in range(5):
-        if inner and t == 2:
-            out(1)
-        if t in (2, 4):
-            make_lists(t, min(5, t + 2), pb[4 if t == 4 else 3])
-        if t not in stat and t < 4:
-            do_pick(t)
-        if t < 4:
-            product(t)
-        else:
-            buf, src, wa, wb, waits = ready(t)
+    def own(t):
+        i = [k for k, (z, j, _e) in enumerate(want) if z == t and j == r][0]
+        if t == 4 or (t == 3 and bound):
             for k in range(2):
-                n1, n2_ = pick(256 * t + 128 * k, wa, wb, T.lu[:, 16 * t + 8 * k:16 * t + 8 * k + 8], nlist[t], buf, src,
-                               waits, 128)
-                stat[t] = (buf, 256 * t, n1, n2_)
+                stat[t] = ("pk", 256 * t) + pick(i, "pk", 256 * t, 8 * k, 8 * k + 8)
                 product(t, (k,))
-        if t > 0 and (t != 2 or not inner):
-            out(t - 1)
-    out(4)
+            return
+        if t not in stat:
+            stat[t] = ("pk", 256 * t) + pick(i, "pk", 256 * t)
+        product(t)
+        if outer:
+            stat[t + 1] = stat[t]
+            product(t + 1)
 
+    def out(t, both=False):
+        o = 256 * t
+        n1 = n2 = 1
+        for k in range(2):
+            e = 512 * ((2 * t + k) % 8)
+            a, b = T.ys[:, o + 128 * k:o + 128 * k + 128], T.acc[:, e:e + 128]
+            if both and k == 0:
+                v.wait_ge(S.ps, 2 * t + 1)
+                n1 = V(v.tensor_copy(a, b))
+            else:
+                sc.wait_ge(S.ps, 2 * t + k + 1)
+                n2 = A(sc.activation(a, b, Act.Copy))
+        copied[t] = (n1, n2)
+        if both:
+            sy.wait_ge(S.vs, n1)
+        sy.wait_ge(S.ss, n2)
+        sy.dma_start(T.y[:, o:o + 256], T.ys[:, o:o + 256]).then_inc(S.st, 16)
+        cst[0] += 16
+
+    def relay(j, w, wait, n, name, es, plane, x=0):
+        g.wait_ge(sem(wait, plane), n)
+        send(plane, w, [(T.cores[partner], es, name, W, col(r, j) + x, W, col(partner, j) + x)])
+
+    low = min(far, key=lambda j: col(r, j))
+
+    U = T.eu
+    v.wait_ge(S.sF, 16)
+    v.wait_ge(S.ke, 4)
+    vw()
+    V(v.tensor_tensor(U[0:64, 0:1], T.ea[0:64, 0:1], T.ea[0:64, 4:5], Op.subtract))
+    vw()
+    V(v.tensor_tensor(U[0:32, 6:7], U[32:64, 0:1], U[0:32, 0:1], Op.is_gt))
+    vw()
+    V(v.tensor_scalar(U[0:32, 32:33], U[0:32, 6:7], float(cp - c0), U[0:32, 2:3], Op.mult, Op.add))
+    vw()
+    turn(0)
+    make_lists(0)
+    if bound:
+        n = pick(0, "px", 0, fr="wq")
+        stat[0] = ("px", 0) + n
+        for plane in (False, True):
+            g.wait_ge(S.ss if plane else S.vs, n[plane])
+            send(plane, 256, [(T.cores[7 - r], off, "x1", "px", 0, "wb", col(7 - r, X1)),
+                              (helper(r), on, "ht", "px", 0, "hx", 0)])
+    else:
+        own(0)
+        out(0)
+        if outer:
+            out(1)
     for plane in (False, True):
-        half_there(v, plane)
-        for name, n in (("x1", nx1), ("x2", noff)) if mid else (("rw", 2 * noff),):
-            v.wait_ge(sem(name, plane), n)
+        if inner or outer:
+            relay(low, 512, "bo", nbo[plane], "br", on, plane)
+        elif bound:
+            relay(X1, 256, "x1", noff, "x1", near, plane)
+
+    def send_x2():
+        make_lists(1)
+        k = of_role(1 - h, BOUND)
+        n = [pick(1, "pa", 0, 8 * i, 8 * i + 8) for i in range(2)]
+        x = col(k, X2)
+        g.wait_ge(S.vs, n[0][0])
+        send(False, 128, [(T.cores[k], off, "x2", "pa", 0, "wb", x)])
+        g.wait_ge(S.ss, n[1][1])
+        send(True, 256, [(T.cores[k], off, "x2", "pa", 0, "wb", x)])
+        g.wait_ge(S.vs, n[1][0])
+        g.remote_dma_fused([RemoteDMATransfer(dst_ids=[dst(T.cores[j]) for j in (k, k ^ 1)], dma_engine_mask=bits(off),
+                                              remote_sem=S.x3, srcs=[view("pa", 128, 128, False)],
+                                              dsts=[view("wb", x + 128, 128, False)] * 2)], local_sem=S.ls)
+        cl[0] += noff
+
+    COL, e = {}, 4
+    for t in (4, 3, 2, 1):
+        COL[t] = e
+        e += 4 * len(PR[t])
+    SIZE = [e, COL[1], COL[2], COL[3]]
+
+    v.wait_ge(S.sO, 16 * len(chips))
+    for t in range(4):
+        a, b = PR[t][0], PR[t][-1] + 1
+        to = T.s0[0:64, COL[t]:COL[t] + 4 * (b - a)] if t else T.e0[0:64, 0:4 * (b - a)]
+        f = 4 * t
+        if t % 2 == 0:
+            V(v.tensor_tensor(to, T.sl[0:64, a:b, f:f + 4], T.sl[64:128, a:b, f:f + 4], Op.subtract))
+        else:
+            V(v.tensor_tensor(to, T.sl[64:128, a:b, f:f + 4], T.sl[0:64, a + 1:b + 1, f:f + 4], Op.subtract))
+    v.wait_ge(S.sP, 16)
+    last = V(v.tensor_tensor(T.s0[0:64, 4:8], T.sm[0:64, 12:16], T.sm[64:128, 12:16], Op.subtract))
+
+    for t in range(4):
+        n, odd = SIZE[t], t % 2
+        n16 = -(-n // 16)
+        lo, np = PR[t][0], len(PR[t])
+        a, b = (T.sab[0:32, 1, 0:n], T.sab[0:32, 0, 1:n + 1]) if odd else (T.sab[0:32, 0, 0:n], T.sab[0:32, 1, 0:n])
+        w = 5 * np - 4
+        cc = T.co if odd else T.ce
+        vw(last)
+        if t == 2 and outer:
+            turn(1)
+        if t:
+            c = COL[t] + lo
+            ea, eb = T.sab[0:32, odd, c:c + w:5], T.sab[0:32, 1 - odd, c + odd:c + odd + w:5]
+            if t < 3 or m < 3:
+                V(v.tensor_tensor(cc[0:32, lo:lo + np], eb, ea, Op.is_gt))
+            if t == 3 and m:
+                V(v.tensor_tensor(T.wk[0:32, 4:5], T.sab[0:32, 0, c + 1:c + 2], T.sab[0:32, 1, c:c + 1], Op.is_le))
+            k = V(v.tensor_tensor(T.dd[0:32, 0:n], b, a, Op.subtract))
+            if t > (2 if outer else 1):
+                turn(t - 1)
+            fa, fb = a, b
+        else:
+            V(v.tensor_tensor(cc[0:32, lo:lo + np], T.e0[32:64, lo:lo + w:5], T.e0[0:32, lo:lo + w:5], Op.is_gt))
+            k = V(v.tensor_tensor(T.dd[0:32, 4:n], T.s0[32:64, 4:n], T.s0[0:32, 4:n], Op.subtract))
+            fa, fb = T.s0[0:32, 0:n], T.s0[32:64, 0:n]
+        if t < 3:
+            vw(k)
+            k = V(v.tensor_tensor(T.cd[:, 0:16 * n16], cc[:, 0:8].indirect(T.of[:, 0:n16]), T.dd[:, 0:16 * n16], Op.mult))
+            if t == 2 and outer:
+                send_x2()
+            vw(k)
+            V(v.tensor_tensor(a, fa, T.cd[0:32, 0:n], Op.add))
+            last = V(v.tensor_tensor(b, fb, T.cd[0:32, 0:n], Op.subtract))
+        else:
+            vw()
+            for i in (4 + m, m):
+                if m < 3:
+                    x = T.sab[0:32, 1, i:i + 1]
+                    last = V(v.tensor_scalar(x, T.dd[0:32, i:i + 1], cc[0:32, m:m + 1], x, Op.mult, Op.add))
+                if m:
+                    last = V(v.tensor_scalar(T.sab[0:32, 0, i:i + 1], T.dd[0:32, i - 1:i], T.wk[0:32, 4:5],
+                                             T.sab[0:32, 1, i - 1:i], Op.mult, Op.add))
+        if t == 1 and bound:
+            own(0)
+            out(0)
+    mine, his = T.sab[0:32, r % 2, m:m + 1], T.sab[0:32, 1 - r % 2, m:m + 1]
+    vw(last)
+    V(v.tensor_tensor(T.wk[0:32, 1:2], T.sab[0:32, 1, 4 + m:5 + m], T.sab[0:32, 0, 4 + m:5 + m], Op.is_gt))
+    k = V(v.tensor_tensor(T.wk[0:32, 2:3], his, mine, Op.subtract))
+    turn(3)
+    vw(k)
+    V(v.tensor_scalar(T.wk[0:32, 0:1], T.wk[0:32, 2:3], T.wk[0:32, 1:2], mine, Op.mult, Op.add))
+    vw()
+    turn(4)
+
+    for i, name in enumerate(("x2",) if bound else ("x1",) if third else ()):
+        for plane in (False, True):
+            relay(X2 if bound else X1, 128 if bound and not plane else 256, name, noff, name, near, plane)
+
+    for s in ("L4 P2 P4 B2 B3 B4" if outer else "L3 P1 L4 P2 B1 P3 B2 P4 B3 B4").split():
+        t = int(s[1])
+        if s[0] == "L":
+            make_lists(t)
+        elif s[0] == "P":
+            own(t)
+        else:
+            out(t, s[0] == "B")
+
     vw()
     sc.wait_ge(S.ss, cs[0])
     te.wait_ge(S.ps, 10)

from concourse.bass import DstId, RemoteDMATransfer
from concourse.mybir import dt, AluOpType as Op, ActivationFunctionType as Act

C8 = "float8_e4m3fn_x4"
SCRATCH = {
    "la": ("dram", [8, 128, 2], "int32"),
    "lb": ("dram", [2, 128, 2], "int32"),
    "wt": ("sbuf", [128, 1024], "bfloat16"),
    "xt": ("sbuf", [128, 2560], "bfloat16"),
    "xq": ("sbuf", [128, 640], C8), "xs": ("sbuf", [128, 640], "uint8"),
    "wq": ("sbuf", [128, 512], C8), "wqs": ("sbuf", [128, 512], "uint8"),
    "wa": ("sbuf", [128, 1280], C8), "was": ("sbuf", [128, 1280], "uint8"),
    "wb": ("sbuf", [128, 1536], C8), "wbs": ("sbuf", [128, 1536], "uint8"),
    "hw": ("sbuf", [128, 512], C8), "hws": ("sbuf", [128, 512], "uint8"),
    "hx": ("sbuf", [128, 256], C8), "hxs": ("sbuf", [128, 256], "uint8"),
    "px": ("sbuf", [128, 256], C8), "pxs": ("sbuf", [128, 256], "uint8"),
    "pa": ("sbuf", [128, 256], C8), "pas": ("sbuf", [128, 256], "uint8"),
    "pk": ("sbuf", [128, 1280], C8), "pks": ("sbuf", [128, 1280], "uint8"),
    "sl": ("sbuf", [128, 4, 16], "int32"), "sm": ("sbuf", [128, 16], "int32"),
    "ea": ("sbuf", [128, 8], "int32"),
    "eu": ("sbuf", [128, 64], "float32"),
    "s0": ("sbuf", [128, 48], "float32"), "e0": ("sbuf", [128, 16], "float32"),
    "sab": ("sbuf", [128, 2, 48], "float32"),
    "dd": ("sbuf", [128, 48], "float32"), "cd": ("sbuf", [128, 48], "float32"),
    "ce": ("sbuf", [128, 8], "float32"), "co": ("sbuf", [128, 8], "float32"),
    "wk": ("sbuf", [128, 32], "float32"), "pp": ("sbuf", [128, 2], "float32"),
    "pi": ("sbuf", [128, 4], "int32"), "pj": ("sbuf", [128, 4], "int32"), "p3": ("sbuf", [128, 4], "int32"),
    "of": ("sbuf", [128, 4], "uint16"),
    "tf": ("sbuf", [128, 160], "float32"), "bf": ("sbuf", [128, 40], "float32"), "lu": ("sbuf", [128, 80], "uint16"),
    "ys": ("sbuf", [128, 1280], "float32"),
    "acc": ("psum", [128, 4096], "float32"),
}
SEMAPHORES = ["sD", "sE", "sF", "ke", "wld", "xld", "l0", "l1", "l2", "l3", "lq", "li", "sO", "sP", "cw", "cws",
              "bp", "bps", "bo", "bos", "br", "brs", "x1", "x1s", "x2", "x2s", "x3", "hs", "hss", "ht", "hts",
              "vs", "gs", "ss", "ps", "st", "ls"]

OUTER, THIRD, INNER, BOUND = 0, 1, 2, 3
X1, X2 = 8, 9


def role(r):
    return min(r, 7 - r)


def of_role(h, k):
    return 7 - k if h else k


def land_of(k):
    return of_role(k // 4, OUTER if role(k) >= INNER else INNER)


def col(r, j):
    k = role(r)
    if j == X1:
        return 512 if k == BOUND else 1024
    if j == X2:
        return 1280 if k >= INNER else 1024
    if k < INNER:
        return 256 * role(j)
    return 256 * (j % 2) + (0 if j // 2 == r // 2 else 512 if k == INNER else 768)


def win(r):
    return "wa" if role(r) < INNER else "wb"


def pairs(r, t):
    m = r // 2
    d = (5 - t) // 2
    return list(range(max(0, m - d), min(2, m + d - 1) + 1)) if t % 2 else list(range(max(0, m - d), min(3, m + d) + 1))


def rank_program(g, core, T, topo):
    S = T.sem
    r = T.rank_of(core)

    def dst(c):
        a = topo.addr(c)
        return DstId(rid=a[0], pnc=a[1])

    def bits(es):
        return sum(1 << e for e in es)

    def sem(name, plane):
        return S[name + ("s" if plane else "")]

    def view(b, c, n, plane):
        return T[b + "s"][:, c:c + n] if plane else T[b][:, c:c + n].bitcast(dt.uint8)

    def helper(k):
        c = T.cores[k]
        return [x for x in topo.cores_of(c) if topo.die(x) != topo.die(c) and topo.may_write(x, T.cores[land_of(k)])][0]

    if r is None:
        for k in range(8):
            if role(k) in (OUTER, BOUND) and core == helper(k):
                j, z = land_of(k), of_role(1 - k // 4, THIRD)
                es = topo.engines(core, T.cores[j])
                n = len(es)
                jobs = [("hs", 2 * n, True, "hw", 0, 512, j, 512, "bo")]
                if role(k) == OUTER:
                    jobs.insert(0, ("hs", n, False, "hw", col(j, k) - 512, 256, j, col(j, k), "bo"))
                else:
                    jobs += [("ht", n, plane, "hx", 0, 256, z, col(z, X1), "x1") for plane in (False, True)]
                for wait, cnt, plane, b, a, w, y, x, name in jobs:
                    g.wait_ge(sem(wait, plane), cnt)
                    ad = topo.addr(T.cores[y])
                    g.remote_dma(view(win(y), x, w, plane), view(b, a, w, plane), sem(name, plane), S.ls, ad[1], ad[0], bits(es))
                g.wait_ge(S.ls, n * len(jobs))
        return

    v, sc, sy, te = g.vector, g.scalar, g.sync, g.tensor
    h, m, ro = r // 4, r // 2, role(r)
    outer, third, inner, bound = ro == OUTER, ro == THIRD, ro == INNER, ro == BOUND
    mid = inner or bound
    W = win(r)
    cv, cg, cs, cl, cst = [0], [0], [0], [0], [0]

    def V(i):
        i.then_inc(S.vs, 1)
        cv[0] += 1
        return cv[0]

    def vw(n=None):
        v.wait_ge(S.vs, n or cv[0])

    def G(i):
        i.then_inc(S.gs, 1)
        cg[0] += 1
        return cg[0]

    def A(i):
        i.then_inc(S.ss, 1)
        cs[0] += 1
        return cs[0]

    partner, land = r ^ 1, land_of(r)
    near = topo.engines(core, T.cores[partner])
    off = topo.engines(core, T.cores[land])
    on = [e for e in near if e not in off]
    non, noff, nall = len(on), len(off), len(near)
    PR = [pairs(r, t) for t in range(5)]

    def send(plane, w, to):
        g.remote_dma_fused([RemoteDMATransfer(dst_ids=[dst(c)], dma_engine_mask=bits(es), remote_sem=sem(sm, plane),
                                              srcs=[view(a, x, w, plane)], dsts=[view(b, y, w, plane)])
                            for c, es, sm, a, x, b, y in to], local_sem=S.ls)
        cl[0] += sum(len(x[1]) for x in to)

    u = 4 * (r % 2)
    sy.dma_start(T.la[r], T.dm[:, 0:16]).then_inc(S.sD, 16)
    sc.dma_start(T.ea[0:64, u:u + 2], T.dm[:, m:m + 8]).then_inc(S.sF, 16)
    sc.dma_start(T.lb[r % 2], T.dm[:, 4:20]).then_inc(S.sE, 16)
    sy.dma_start(T.wt[:], T.w[:]).then_inc(S.wld, 16)
    sy.dma_start(T.xt[:], T.x[:]).then_inc(S.xld, 16)

    def first(j):
        return col(r, j if j // 4 == h else X1 if role(j) == BOUND else X2)

    G(g.iota(T.pi[:], [[0, 4]], 0, 1))
    for s in range(2):
        if s:
            g.wait_ge(S.gs, cg[0])
        for k in (0, 2):
            a, b = first(2 * k + s), first(2 * k + 2 + s)
            G(g.iota(T.s0[32 * s:32 * s + 32, k:k + 2], [[b - a, 2]], a, 8, allow_small_or_imprecise_dtypes=True))
    nconst = cg[0]
    ne = V(v.memset(T.ea[64:128, u:u + 4], 0))
    V(v.memset(T.sl[:], 0))
    nz = V(v.memset(T.sm[:], 0))
    for b in ("sab", "ce", "co", "wk", "eu"):
        V(v.memset(T[b][:], 0.0))
    V(v.memset(T.dd[:, 4:48], 0.0))
    for k in range(4):
        V(v.memset(T.dd[:, k:k + 1], float(first(2 * k + 1) - first(2 * k)) if k // 2 == h else 0.0))
    v.wait_ge(S.gs, nconst)
    V(v.tensor_scalar(T.pj[:], T.pi[:], 15, None, Op.bitwise_and))
    V(v.tensor_scalar(T.p3[:], T.pi[:], 3, None, Op.bitwise_and))
    vw()
    V(v.tensor_copy(T.pp[:, 0:1], T.pj[:, 0:1]))
    V(v.tensor_scalar(T.pp[:, 1:2], T.pj[:, 0:1], 16.0, None, Op.add))
    V(v.tensor_copy(T.of[:], T.p3[:]))
    V(v.tensor_copy(T.eu[0:32, 2:3], T.s0[32 * (r % 2):32 * (r % 2) + 32, m:m + 1]))

    def lists(ks, es, sm, b):
        cl[0] += len(es)
        return RemoteDMATransfer(dst_ids=[dst(T.cores[k]) for k in ks], dma_engine_mask=bits(es), remote_sem=sm,
                                 srcs=[b], dsts=[b for k in ks])

    for sm in (S.sD, S.sE, S.sF):
        g.wait_ge(sm, 16)
    g.wait_ge(S.vs, ne)
    lsem = S["l%d" % m]
    far = [k for k in range(8) if k // 4 == h and k // 2 != m]
    to = [k for k in range(8) if k != r and m in pairs(k, 0)]
    g.remote_dma_fused([lists([k], [e], lsem, T.la[r]) for k, e in zip(to, off)]
                       + [lists([partner], off[-1:], S.lq, T.lb[r % 2]), lists([partner], on[0:4], S.ke, T.ea[:, u:u + 2])],
                       local_sem=S.ls)

    c0, cp, cz = col(r, r), col(r, partner), col(land, r)
    src = "wq" if mid else W
    v.wait_ge(S.wld, 16)
    nq = V(v.quantize_mx(T[src][:, c0:c0 + 256], T[src + "s"][:, c0:c0 + 256], T.wt[:]))
    if mid:
        V(v.quantize_mx(T.wb[:, c0:c0 + 256], T.wbs[:, c0:c0 + 256], T.wt[:]))
    g.wait_ge(S.vs, nq)
    for plane in (False, True):
        to = [(T.cores[partner], on[4 * i:4 * i + 4], "bp", src, c0 + 128 * i, "wq" if inner else W, c0 + 128 * i)
              for i in range(2)]
        if outer or plane:
            to += [(helper(r), off[4 * i:4 * i + 4], "hs", src, c0 + 128 * i, "hw", cz - 512 + 128 * i) for i in range(2)]
        else:
            to += [(T.cores[land], off, "bo", src, c0, win(land), cz)]
        send(plane, 128, to)
    if not outer:
        g.wait_ge(S.li, 2)
        send(False, 128, [(T.cores[land], off, "bo", src, c0 + 128, win(land), cz + 128)])

    v.wait_ge(S.xld, 16)
    V(v.quantize_mx(T.xq[:, 0:512], T.xs[:, 0:512], T.xt[:, 0:2048]))
    nx = V(v.quantize_mx(T.xq[:, 512:640], T.xs[:, 512:640], T.xt[:, 2048:2560]))

    chips = sorted(PR[0], key=lambda k: (k != m, k // 2 != h))
    for q in (sy, sc):
        q.wait_ge(S.vs, nz)
    sy.wait_ge(S.sD, 16)
    sc.wait_ge(S.sE, 16)
    sc.wait_ge(S.lq, 1)
    sc.dma_start(T.sm[0:128:4, :], T.lb[:]).then_inc(S.sP, 16)
    for i, k in enumerate(chips):
        q = (sy, sy, sc, sy)[i]
        q.wait_ge(S["l%d" % k], 1 if k == m else 2)
        q.dma_start(T.sl[0:128:4, k, :], T.la[2 * k:2 * k + 2]).then_inc(S.sO, 16)
    if not outer:
        sy.sem_inc(S.li, 1)
        sc.sem_inc(S.li, 1)
    if bound:
        for plane in (False, True):
            sy.wait_ge(sem("bp", plane), non)
            sy.dma_start(view("wb", cp, 256, plane), view("wq", cp, 256, plane)).then_inc(sem("cw", plane), 16)

    nbo = [4 * noff if outer else 3 * noff, noff]
    parts = [[(512, "bp", non), (1024, "bo", 0), (1280, "x1", nall)],
             [(512, "bp", non), (1024, "br", non), (1280, "x1", noff)],
             [(512, "bp", non), (1024, "bo", 0), (1280, "x1", nall), (1408, "x2", nall), (1536, "x3", noff)],
             [(512, "bp", non), (768, "cw", 16), (768, "x1", noff), (1280, "br", non), (1408, "x2", noff),
              (1536, "x3", noff)]][ro]
    want = [[(0, r, 512), (1, land, 1024), (2, r, 1024), (4, r, 1280)],
            [(0, r, 512), (1, r, 1024), (2, r, 1024), (3, r, 1280), (4, r, 1280)],
            [(0, r, 512), (1, r, 1024), (2, r, 1280), (3, r, 1280), (4, r, 1536)],
            [(0, r, 512), (1, r, 768), (2, r, 1280), (3, r, 1536), (4, r, 1536)]][ro]
    groups = {0: (0, 1), 1: (1, 2), 4: (2, 4)} if outer else {0: (0, 1), 3: (1, 4), 4: (4, 5)}
    seen = {}

    def there(q, end, plane):
        for e, name, n in parts:
            if e <= end and (name, plane) not in seen and (name, plane) != ("x3", True):
                q.wait_ge(sem(name, plane), n or nbo[plane])
                seen[(name, plane)] = 1

    nlist, pb, stat, copied = {}, {}, {}, {}

    def pick(i, buf, x, a=0, b=16, fr=W):
        end, lt, w = want[i][2], T.lu[:, 16 * i + a:16 * i + b], 16 * (b - a)
        x += 16 * a
        if end == 1536 and b == 8:
            end -= 128
        vw(nlist[i])
        there(v, end, False)
        n1 = V(v.tensor_copy(T[buf][:, x:x + w].bitcast(dt.uint32), T[fr][:, 0:end].bitcast(dt.uint32).indirect(lt)))
        sc.wait_ge(S.vs, nlist[i])
        there(sc, end, True)
        return n1, A(sc.activation(T[buf + "s"][:, x:x + w], T[fr + "s"][:, 0:end].indirect(lt), Act.Copy))

    def turn(t):
        for i, (z, j, _e) in enumerate(want):
            if z == t:
                fr = T.wk[0:32, :] if t == 4 else T.sab[0:32, j % 2, j // 2:j // 2 + 32] if t else T.eu[0:32, 32:64]
                k = V(v.transpose(T.tf[0:32, 32 * i:32 * i + 32], fr))
        if t in groups:
            a, b = groups[t]
            g.wait_ge(S.vs, k)
            pb[t] = G(g.partition_broadcast(T.bf[0:128, 8 * a:8 * b], T.tf[0:1, 32 * a:32 * b:4], 128))

    def make_lists(t):
        a, b = groups[t]
        v.wait_ge(S.gs, pb[t])
        fr = T.bf[:, 8 * a:8 * b]
        V(v.tensor_scalar(T.lu[:, 16 * a:16 * b:2], fr, T.pp[:, 0:1], None, Op.add))
        n = V(v.tensor_scalar(T.lu[:, 16 * a + 1:16 * b:2], fr, T.pp[:, 1:2], None, Op.add))
        for i in range(a, b):
            nlist[i] = n

    def product(t, ks=(0, 1)):
        buf, x, n1, n2 = stat[t]
        te.wait_ge(S.vs, max(n1, nx))
        te.wait_ge(S.ss, n2)
        if t == 4:
            te.wait_ge(S.vs, copied[0][0])
            te.wait_ge(S.ss, copied[0][1])
        for k in ks:
            e = 512 * ((2 * t + k) % 8)
            c = x + 128 * k
            te.matmul_mx(T.acc[:, e:e + 128], T[buf][:, c:c + 128], T[buf + "s"][:, c:c + 128],
                         T.xq[:, 128 * t:128 * t + 128], T.xs[:, 128 * t:128 * t + 128], True, True).then_inc(S.ps, 1)

    def own(t):
        i = [k for k, (z, j, _e) in enumerate(want) if z == t and j == r][0]
        if t == 4 or (t == 3 and bound):
            for k in range(2):
                stat[t] = ("pk", 256 * t) + pick(i, "pk", 256 * t, 8 * k, 8 * k + 8)
                product(t, (k,))
            return
        if t not in stat:
            stat[t] = ("pk", 256 * t) + pick(i, "pk", 256 * t)
        product(t)
        if outer:
            stat[t + 1] = stat[t]
            product(t + 1)

    def out(t, both=False):
        o = 256 * t
        n1 = n2 = 1
        for k in range(2):
            e = 512 * ((2 * t + k) % 8)
            a, b = T.ys[:, o + 128 * k:o + 128 * k + 128], T.acc[:, e:e + 128]
            if both and k == 0:
                v.wait_ge(S.ps, 2 * t + 1)
                n1 = V(v.tensor_copy(a, b))
            else:
                sc.wait_ge(S.ps, 2 * t + k + 1)
                n2 = A(sc.activation(a, b, Act.Copy))
        copied[t] = (n1, n2)
        if both:
            sy.wait_ge(S.vs, n1)
        sy.wait_ge(S.ss, n2)
        sy.dma_start(T.y[:, o:o + 256], T.ys[:, o:o + 256]).then_inc(S.st, 16)
        cst[0] += 16

    def relay(j, w, wait, n, name, es, plane, x=0):
        g.wait_ge(sem(wait, plane), n)
        send(plane, w, [(T.cores[partner], es, name, W, col(r, j) + x, W, col(partner, j) + x)])

    low = min(far, key=lambda j: col(r, j))

    U = T.eu
    v.wait_ge(S.sF, 16)
    v.wait_ge(S.ke, 4)
    vw()
    V(v.tensor_tensor(U[0:64, 0:1], T.ea[0:64, 0:1], T.ea[0:64, 4:5], Op.subtract))
    vw()
    V(v.tensor_tensor(U[0:32, 6:7], U[32:64, 0:1], U[0:32, 0:1], Op.is_gt))
    vw()
    V(v.tensor_scalar(U[0:32, 32:33], U[0:32, 6:7], float(cp - c0), U[0:32, 2:3], Op.mult, Op.add))
    vw()
    turn(0)
    make_lists(0)
    if bound:
        n = pick(0, "px", 0, fr="wq")
        stat[0] = ("px", 0) + n
        for plane in (False, True):
            g.wait_ge(S.ss if plane else S.vs, n[plane])
            send(plane, 256, [(T.cores[7 - r], off, "x1", "px", 0, "wb", col(7 - r, X1)),
                              (helper(r), on, "ht", "px", 0, "hx", 0)])
    else:
        own(0)
        out(0)
        if outer:
            out(1)
    for plane in (False, True):
        if inner or outer:
            relay(low, 512, "bo", nbo[plane], "br", on, plane)
        elif bound:
            relay(X1, 256, "x1", noff, "x1", near, plane)

    def send_x2():
        make_lists(1)
        k = of_role(1 - h, BOUND)
        n = [pick(1, "pa", 0, 8 * i, 8 * i + 8) for i in range(2)]
        x = col(k, X2)
        g.wait_ge(S.vs, n[0][0])
        send(False, 128, [(T.cores[k], off, "x2", "pa", 0, "wb", x)])
        g.wait_ge(S.ss, n[1][1])
        send(True, 256, [(T.cores[k], off, "x2", "pa", 0, "wb", x)])
        g.wait_ge(S.vs, n[1][0])
        g.remote_dma_fused([RemoteDMATransfer(dst_ids=[dst(T.cores[j]) for j in (k, k ^ 1)], dma_engine_mask=bits(off),
                                              remote_sem=S.x3, srcs=[view("pa", 128, 128, False)],
                                              dsts=[view("wb", x + 128, 128, False)] * 2)], local_sem=S.ls)
        cl[0] += noff

    COL, e = {}, 4
    for t in (4, 3, 2, 1):
        COL[t] = e
        e += 4 * len(PR[t])
    SIZE = [e, COL[1], COL[2], COL[3]]

    v.wait_ge(S.sO, 16 * len(chips))
    for t in range(4):
        a, b = PR[t][0], PR[t][-1] + 1
        to = T.s0[0:64, COL[t]:COL[t] + 4 * (b - a)] if t else T.e0[0:64, 0:4 * (b - a)]
        f = 4 * t
        if t % 2 == 0:
            V(v.tensor_tensor(to, T.sl[0:64, a:b, f:f + 4], T.sl[64:128, a:b, f:f + 4], Op.subtract))
        else:
            V(v.tensor_tensor(to, T.sl[64:128, a:b, f:f + 4], T.sl[0:64, a + 1:b + 1, f:f + 4], Op.subtract))
    v.wait_ge(S.sP, 16)
    last = V(v.tensor_tensor(T.s0[0:64, 4:8], T.sm[0:64, 12:16], T.sm[64:128, 12:16], Op.subtract))

    for t in range(4):
        n, odd = SIZE[t], t % 2
        n16 = -(-n // 16)
        lo, np = PR[t][0], len(PR[t])
        a, b = (T.sab[0:32, 1, 0:n], T.sab[0:32, 0, 1:n + 1]) if odd else (T.sab[0:32, 0, 0:n], T.sab[0:32, 1, 0:n])
        w = 5 * np - 4
        cc = T.co if odd else T.ce
        vw(last)
        if t == 2 and outer:
            turn(1)
        if t:
            c = COL[t] + lo
            ea, eb = T.sab[0:32, odd, c:c + w:5], T.sab[0:32, 1 - odd, c + odd:c + odd + w:5]
            if t < 3 or m < 3:
                V(v.tensor_tensor(cc[0:32, lo:lo + np], eb, ea, Op.is_gt))
            if t == 3 and m:
                V(v.tensor_tensor(T.wk[0:32, 4:5], T.sab[0:32, 0, c + 1:c + 2], T.sab[0:32, 1, c:c + 1], Op.is_le))
            k = V(v.tensor_tensor(T.dd[0:32, 0:n], b, a, Op.subtract))
            if t > (2 if outer else 1):
                turn(t - 1)
            fa, fb = a, b
        else:
            V(v.tensor_tensor(cc[0:32, lo:lo + np], T.e0[32:64, lo:lo + w:5], T.e0[0:32, lo:lo + w:5], Op.is_gt))
            k = V(v.tensor_tensor(T.dd[0:32, 4:n], T.s0[32:64, 4:n], T.s0[0:32, 4:n], Op.subtract))
            fa, fb = T.s0[0:32, 0:n], T.s0[32:64, 0:n]
        if t < 3:
            vw(k)
            k = V(v.tensor_tensor(T.cd[:, 0:16 * n16], cc[:, 0:8].indirect(T.of[:, 0:n16]), T.dd[:, 0:16 * n16], Op.mult))
            if t == 2 and outer:
                send_x2()
            vw(k)
            V(v.tensor_tensor(a, fa, T.cd[0:32, 0:n], Op.add))
            last = V(v.tensor_tensor(b, fb, T.cd[0:32, 0:n], Op.subtract))
        else:
            vw()
            for i in (4 + m, m):
                if m < 3:
                    x = T.sab[0:32, 1, i:i + 1]
                    last = V(v.tensor_scalar(x, T.dd[0:32, i:i + 1], cc[0:32, m:m + 1], x, Op.mult, Op.add))
                if m:
                    last = V(v.tensor_scalar(T.sab[0:32, 0, i:i + 1], T.dd[0:32, i - 1:i], T.wk[0:32, 4:5],
                                             T.sab[0:32, 1, i - 1:i], Op.mult, Op.add))
        if t == 1 and bound:
            own(0)
            out(0)
    mine, his = T.sab[0:32, r % 2, m:m + 1], T.sab[0:32, 1 - r % 2, m:m + 1]
    vw(last)
    V(v.tensor_tensor(T.wk[0:32, 1:2], T.sab[0:32, 1, 4 + m:5 + m], T.sab[0:32, 0, 4 + m:5 + m], Op.is_gt))
    k = V(v.tensor_tensor(T.wk[0:32, 2:3], his, mine, Op.subtract))
    turn(3)
    vw(k)
    V(v.tensor_scalar(T.wk[0:32, 0:1], T.wk[0:32, 2:3], T.wk[0:32, 1:2], mine, Op.mult, Op.add))
    vw()
    turn(4)

    for i, name in enumerate(("x2",) if bound else ("x1",) if third else ()):
        for plane in (False, True):
            relay(X2 if bound else X1, 128 if bound and not plane else 256, name, noff, name, near, plane)

    for s in ("L4 P2 P4 B2 B3 B4" if outer else "L3 P1 L4 P2 B1 P3 B2 P4 B3 B4").split():
        t = int(s[1])
        if s[0] == "L":
            make_lists(t)
        elif s[0] == "P":
            own(t)
        else:
            out(t, s[0] == "B")

    vw()
    sc.wait_ge(S.ss, cs[0])
    te.wait_ge(S.ps, 10)
    sy.wait_ge(S.st, cst[0])
    g.wait_ge(S.gs, cg[0])
    g.wait_ge(S.ls, cl[0])
